import numpy as np, ml_dtypes
CORES = [48,51,52,55]
N = 4
BF = ml_dtypes.bfloat16
S, L, R, B, CAP = 8, 256, 6, 2304, 64
A, W = S * L, B + R * L
def parts(rng):
    x = rng.integers(0, 256, (N, 8, 16, B)); k = rng.integers(0, B, (N, 8, 16, B))
    head = rng.integers(0, B, (N, 8, 6, 64)); clan = rng.integers(0, 64, (N, 8, 1, B))
    k[:, :, :6] = np.where(rng.random((N, 8, 6, B)) < 0.35, np.take_along_axis(head, np.repeat(clan, 6, axis=2), 3), k[:, :, :6])
    return x, k, rng.integers(800, 1201, (N, 8, R)), rng.integers(0, 256, (N, 8, 16, R))
def pack(x, k, th, w):
    return {"xf": np.ascontiguousarray(x.reshape(N, 128, B)).astype(np.float32).astype(BF), "kin": np.ascontiguousarray(k.reshape(N, 128, B)).astype(np.int32),
            "th": np.ascontiguousarray(th).astype(np.int32), "w": np.ascontiguousarray(w.reshape(N, 128, R)).astype(np.int32)}
def setup_inputs(rng):
    return pack(*parts(rng))
def setup_inputs_spread(rng):
    x, k, th, w = parts(rng)
    size = np.exp2(8 * rng.random((N, 8, 1, B))) * (rng.random((N, 8, 1, B)) > 0.0625)
    x = np.minimum((size * rng.random(x.shape)).astype(np.int64), 255)
    few = np.minimum((B * rng.random(k.shape) ** rng.choice(np.array([1.0, 2.0, 4.0]), (N, 8, 1, 1))).astype(np.int64), B - 1)
    k = np.where(rng.random(k.shape) < 0.5, few, k)
    th = np.minimum(np.exp2(4 + 8 * rng.random(th.shape)).astype(np.int64), 4095)
    w = np.minimum((np.exp2(8 * rng.random((N, 8, 1, R))) * rng.random(w.shape)).astype(np.int64), 255)
    return pack(x, k, th, w)
def setup_inputs_ends(rng):
    x, k, th, w = parts(rng)
    kind = rng.integers(0, 3, (N, 8, 1, B)); x = 255 * np.where(kind == 2, rng.integers(0, 2, x.shape), kind)
    loose = rng.random((N, 8, 1, B)) < 0.2; loose[..., 0] = True; loose[..., B - 1] = True
    k[:, 7] = rng.integers(0, B - 32, (N, 16, B))
    end = (B - 1) * rng.integers(0, 2, k.shape); k = np.where(loose, k, end)
    top = np.arange(B - 32, B - 2); top = top[(top & (S - 1)) != 0][-16:]; last = S * (L - 1) + np.arange(R)
    kg, xg = k[:, 7], x[:, 7]
    mid = S * np.arange(CAP // 2, L - 1) + 1; xg[:, :, mid] = 255
    kg[:, :, last] = B - 2; xg[:, :, last] = 0; xg[:, :, top] = 255; kg[:, :, top] = end[:, 7][:, :, top]
    for q in range(N): kg[q, :, B - 2] = rng.permutation(top)
    th = 4095 * rng.integers(0, 2, th.shape); th[:, 7] = 4095 * ((np.arange(R) + 1) & 1)
    w = 255 * rng.integers(0, 2, w.shape); w[:, 7] = 255
    return pack(x, k, th, w)
def setup_inputs_corners(rng):
    x, k, th, w = parts(rng); i = np.arange(L); v = S * i; u = v + 1; mm = v + 2; own = np.arange(B)
    z = rng.integers(0, 6, (N, 4, 16, B)); k[:, 1::2] = np.where(z == 0, 0, np.where(z == 1, B - 1, np.where(z == 2, own, k[:, 1::2])))
    e = k[..., mm]; k[..., mm] = e + ((e & (S - 1)) == 1)
    th = rng.choice(np.array([0, 1, 700, 1000, 1100, 4095]), th.shape); w = rng.choice(np.array([0, 1, 128, 255]), w.shape)
    for q in range(N):
        for g in range(8):
            F = int(rng.choice(np.array([0, 1, CAP - 1, CAP, CAP + 1, L])))
            if q == 0: F = (0, 1, CAP - 1, CAP, CAP + 1, L, CAP, L)[g]
            must = q == 0 and g == 3
            lose = np.zeros(L, bool); o = rng.permutation(L)
            if must: o = np.concatenate([np.array([0]), 1 + rng.permutation(L - 2), np.array([L - 1])])
            lose[o[:F]] = True
            if q == N - 1 and g == 7: lose = i >= L - CAP
            t0 = int(rng.choice(np.array([1, 17, 300, 2399]))); how = rng.integers(0, 4, L)
            if must: how[0] = 1
            far0 = np.where(lose & (how == 3), t0, np.where(rng.random(L) < 0.5, t0 - 1, rng.integers(0, t0, L)))
            kg, xg = k[q, g], x[q, g]; base = rng.integers(0, 100, (16, L))
            xg[:, v] = base; xg[:, mm] = base + far0 // 16 + (np.arange(16)[:, None] < (far0 & 15))
            src = np.nonzero(~lose | (how == 3))[0]; at = np.searchsorted(src, i); goal = mm.copy()
            named = lose & (how == 2) & (at > 0); none = lose & ((how == 0) | ((how == 2) & (at == 0))); blood = lose & (how == 1)
            bl, wl = np.nonzero(blood)[0], np.nonzero(~lose)[0]
            if must: bl, wl = bl[1:], wl[:-1]
            pairs = min(len(bl), len(wl)); bl = bl[np.argsort(rng.random(len(bl)))[:pairs]]; wl = wl[np.argsort(rng.random(len(wl)))[:pairs]]
            ok = bl < wl; bl, wl = bl[ok], wl[ok]
            if must: bl, wl = np.append(bl, 0), np.append(wl, L - 1)
            goal[wl] = mm[bl]; xg[:, v[wl]] = xg[:, goal[wl]]
            j = (rng.random(L) * at).astype(np.int64)
            if np.any(named):
                goal[named] = goal[src[j[named]]]; xg[:, v[named]] = xg[:, goal[named]]
            goal[none] = np.where(rng.random(L) < 0.5, v, S * rng.integers(0, L, L))[none]
            kg[:, v] = u; kg[:, u] = goal; row = rng.integers(0, 6, L); kg[row[blood], mm[blood]] = u[blood]
            th[q, g, 0] = t0
    return pack(x, k, th, w)
def setup_inputs_ties(rng):
    x, k, th, w = parts(rng); x = rng.integers(0, 3, x.shape); x[:, 1::2] = rng.integers(0, 2, (N, 4, 16, B))
    crowd = rng.integers(0, B, (N, 8, 48)); j = rng.integers(0, 48, (N, 8, 16 * B))
    c = np.take_along_axis(crowd, j, 2).reshape(k.shape); m = rng.random(k.shape) < 0.6; m[:, 1::2] = False; k = np.where(m, c, k)
    th = rng.integers(3, 13, th.shape); one = int(rng.integers(0, 8)); x[:, one] = 255; th[:, one] = rng.integers(0, 2, (N, R))
    return pack(x, k, th, w)
def court(rng, xg, kg, t, goal, d):
    v = S * np.arange(L) + t; u = S * rng.permutation(L) + 3; base = rng.integers(0, 240, (16, L))
    xg[:, v] = base; xg[:, goal] = base + d // 16 + (np.arange(16)[:, None] < (d & 15))
    kg[8, v] = u; kg[(8 + t) & 15, u] = goal
def setup_inputs_turns(rng):
    x, k, th, w = parts(rng); own = np.arange(B); o = int(rng.integers(0, N)); towns = rng.permutation(8)[:4]; row = np.arange(16)[:, None]
    for full in range(2):
        q = (o + full) % N; t = 2 - full
        k[q, :, :6] = (k[q, :, :6] & -2) | (own & 1)
        count = 16 * rng.integers(1, 5, 8); count[int(rng.integers(0, 8))] += 15
        if full: count[:] = L
        th[q, :, 1] = 0
        for g in range(8):
            a, b = int(rng.integers(17, 100)), int(rng.integers(17, 100))
            d = np.where(rng.permutation(L) < count[g], rng.integers(0, a, L), a + rng.integers(0, 15, L))
            court(rng, x[q, g], k[q, g], 0, S * rng.permutation(L) + 3, d)
            d = np.where(rng.random(L) < 0.5, b - 1, b + rng.integers(0, 15, L))
            court(rng, x[q, g], k[q, g], t, S * rng.permutation(L) + 1 + full, d)
            th[q, g, 0] = a; th[q, g, t] = b
    for j in range(2, N):
        q = (o + j) % N
        for g in towns:
            xg, kg = x[q, g], k[q, g]
            high = int(rng.integers(200, 235)); y = rng.integers(0, 21, (8, B))
            xg[0::2] = high + y; xg[1::2] = high - y; xg += row < rng.integers(0, 16, B)
            low = int(rng.integers(20, 50)); y = rng.integers(0, 20, (8, L)); tight = np.zeros((16, L), np.int64)
            tight[0::2] = low + y; tight[1::2] = low - y; tight += row < rng.integers(0, 4, L)
            loose = np.clip(rng.integers(0, 71, L) + rng.integers(-8, 9, (16, L)), 0, 70)
            xg[:, S * np.arange(L)] = np.where(rng.random(L) < 0.5, tight, loose)
            kg += (kg & (S - 1)) == 0
            th[q, g, 0] = 16 * (high - low)
    return pack(x, k, th, w)
def check_inputs(d):
    bad = []
    for a, lo, hi in (("xf", 0, 255), ("kin", 0, B - 1), ("th", 0, 4095), ("w", 0, 255)):
        b = np.asarray(d[a]).astype(np.float64)
        if not (np.min(b) >= lo and np.max(b) <= hi): bad.append("range of " + a)
        if np.any(b != np.floor(b)): bad.append("whole numbers in " + a)
    return bad
def pick(a, ix):
    return np.stack([np.stack([np.take(a[q, g], ix[q, g], axis=1) for g in range(8)]) for q in range(N)])
def score(xc, xv):
    return np.add.reduce(np.abs(xc - xv[:, :, :, None, :]), axis=2)
def reference(xf, kin, th, w):
    X = np.zeros((N, 8, 16, W), np.int32); X[..., :B] = xf.astype(np.float32).reshape(N, 8, 16, B).astype(np.int32)
    K = np.zeros((N, 8, 16, W), np.int32); K[..., :B] = kin.reshape(N, 8, 16, B)
    wt = w.astype(np.int32).reshape(N, 8, 16, R); lane = np.arange(L, dtype=np.int32); last = np.zeros(N, np.int32)
    qa = np.arange(N).reshape(N, 1, 1, 1); ga = np.arange(8).reshape(1, 8, 1, 1); ka = np.arange(16).reshape(1, 1, 16, 1)
    for t in range(R):
        v = S * lane + t; n = B + L * t + lane; kv = K[..., v]; xv = X[..., v]
        c = K[qa, ga, (ka + t) & 15, kv]
        bar = ((c & (S - 1)) == t) | np.any(pick(K[:, :, :6], c) == kv[:, :, :6, None, :], axis=2)
        s = np.where(bar, 1000000, score(pick(X, c), xv))
        best = np.argmin(s, axis=2); low = np.min(s, axis=2); some = low < 1000000
        m = np.where(some, np.take_along_axis(c, best[:, :, None, :], 2)[:, :, 0], -1 - lane)
        taken = np.any((m[..., :, None] == m[..., None, :]) & (lane[:, None] > lane[None, :]), axis=3)
        wed = some & ~taken & (low < th[:, :, t][:, :, None] + (last & 15)[:, None, None])
        last = np.add.reduce(np.add.reduce(wed.astype(np.int32), axis=2), axis=1)
        ms = np.where(wed, m, v); km = pick(K, ms); xm = pick(X, ms)
        vb = np.broadcast_to(v, (N, 8, 1, L)); nb = np.broadcast_to(n, (N, 8, 1, L))
        child = np.concatenate([vb, ms[:, :, None, :], kv[:, :, 0:2], km[:, :, 0:2], nb, nb, kv[:, :, 7:8], km[:, :, 9:16]], axis=2)
        lost = (~wed).astype(np.int32); ask = ~wed & (np.add.accumulate(lost, axis=2) - lost < CAP)
        far = 1 + t % (N - 1); Kq = np.roll(K, -far, axis=0); Xq = np.roll(X, -far, axis=0)
        a = np.add.reduce(wt[..., t][..., None] * xv, axis=2) & (A - 1)
        cx = pick(Xq, pick(Kq, a)); bq = np.argmin(score(cx, xv), axis=2)
        near = np.take_along_axis(cx, bq[:, :, None, None, :], 3)[:, :, :, 0]
        X[..., n] = np.where(wed[:, :, None], (xv + xm) >> 1, np.where(ask[:, :, None], near, xv))
        K[..., n] = np.where(wed[:, :, None], child, kv)
        K[:, :, 6, v] = np.where(wed, m, kv[:, :, 6]); K[:, :, 7, v] = np.where(wed, n, kv[:, :, 7]); K[:, :, 9 + t, v] = np.where(ask, n, kv[:, :, 9 + t])
        qi, gi, li = np.nonzero(wed); mi = m[qi, gi, li]; K[qi, gi, 6, mi] = v[li]; K[qi, gi, 7, mi] = n[li]
    return {"yk": K.reshape(N, 128, W).astype(np.float32), "yx": np.ascontiguousarray(X[..., B:]).reshape(N, 128, R * L).astype(np.float32).astype(BF)}

@@ -1,0 +1,781 @@
+from concourse.mybir import AluOpType as ALU, AxisListType as AX, ActivationFunctionType as AF
+
+N, R, L, B, W = 4, 6, 256, 2304, 3840
+F32, BF, F16, I32, U16 = "float32", "bfloat16", "float16", "int32", "uint16"
+SZ = {F32: 4, BF: 2, F16: 2, I32: 4, U16: 2}
+EW = 8128.0
+MAG0 = 12582912.0
+BIG = 16777216.0
+
+ROUTE = {"S": "aaaa", "D": "aaad"}
+ACT16 = True
+HF = F16 if ACT16 else F32
+ADVE = {"S": 0, "D": 1}
+
+SB = {
+    "kint": ([128, B], I32), "K0": ([128, B], F32), "K": ([128, W + L], F32), "KB": ([128, W], F32),
+    "X": ([128, W], BF), "XQ1": ([128, W - L], BF), "XQ2": ([128, W - L], BF), "XQ3": ([128, W - L], BF),
+    "kvb0": ([128, 2048], F32), "kvb1": ([128, 2048], F32), "xvb0": ([128, 2048], BF), "xvb1": ([128, 2048], BF),
+    "pI": ([128, 8], I32), "pF": ([128, 16], F32), "J": ([128, 256], F32), "JB": ([128, 256], F32),
+    "J16": ([128, 256], F16), "RM": ([128, 16], F32), "Blk": ([128, 16], F32), "Blk16": ([128, 8], F16), "IW": ([128, 176], F32),
+    "Ib": ([128, 128], BF), "nIb": ([128, 128], BF), "hIb": ([128, 128], BF), "oneb": ([128, 128], BF),
+    "Dm": ([128, 256], BF), "wt": ([128, 256], F32), "Mm": ([128, 256], BF), "repl": ([128, 16], U16),
+    "RR": ([128, 64], BF), "RE": ([128, 192], BF), "CE": ([128, 64], F32), "tmpc": ([128, 512], F32),
+    "MA": ([128, 176], F16), "MB": ([128, 256], F32), "MC": ([128, 176], F32),
+    "W32": ([128, 16 if ACT16 else 16 * 144], F32), "W16": ([128, 16 * 144], F16), "QW": ([128, 4 * 176], BF),
+    "kc": ([128, 512], F16), "one16": ([128, 128], F16), "kca": ([128, 128], F16), "qc": ([128, 256], BF),
+    "CM": ([128, 6 * 128], F16), "CA": ([128, 6 * 128], F16), "BI": ([128, 32], F32),
+    "wI": ([128, 8], I32), "wF": ([128, 8], F32), "wS": ([128, 48], BF), "thI": ([128, 48], I32), "thF": ([128, 48], F32),
+    "thB": ([128, 48], F32), "thz": ([128, 16], F32), "zF": ([128, 8], F32), "zI": ([128, 8], I32),
+    "aI": ([128, 96], I32), "aJ": ([128, 96], I32), "aL": ([128, 256], F16), "aU": ([128, 96], U16),
+    "aR": ([128, 96], U16), "dS": ([128, R * L], F32), "dR": ([128, R * L], F32),
+    "scn": ([128, 512], F32), "rst": ([128, 512], F32),
+    "kI": ([128, 32], I32), "kJ": ([128, 32], I32), "sm": ([128, 160], F32), "mT": ([128, 16], F32), "nk": ([128, 16], BF),
+    "lost": ([128, 16], F32), "LM": ([128, 256], F16), "LR": ([128, 256], HF), "IH": ([128, 128], HF), "mW": ([128, 16], F32),
+    "mR": ([128, 256], F16), "E": ([128, 16 * 256], BF), "Lw": ([128, 256], BF), "Lr": ([128, 256], BF),
+    "uL": ([128, 96], U16), "kv16": ([128, 256], F16), "km16": ([128, 256], F16), "xm": ([128, 256], BF),
+    "KW": ([128, 768], F32), "SW": ([128, 768], F32), "XW": ([128, 832], BF), "kmN": ([128, 256], F32),
+    "pk": ([128, 256], F32), "pc": ([128, 512], F32), "pr": ([128, 64], F32), "xc": ([128, 64], BF), "dU": ([128, 64], U16),
+    "Xa": ([128, 1024], BF), "Da": ([128, 1024], BF), "asn": ([128, 128], F32), "bI": ([128, 8], I32), "bJ": ([128, 8], I32),
+    "bL": ([128, 128], F16), "nBR": ([128, 128], F16),
+}
+for _s in "SD":
+    if not ACT16:
+        SB["G32" + _s] = ([128, 2048], F32)
+    if ACT16 or ADVE[_s]:
+        SB["G16" + _s] = ([128, 2048 if ACT16 else 1024 * ADVE[_s]], F16)
+    for _n, _d in (("Xc", BF), ("Dab", BF), ("Dsg", BF), ("eq", BF)):
+        if _n != "Dsg" or "d" in ROUTE[_s]:
+            SB[_n + _s] = ([128, 2048], _d)
+    SB["l1" + _s] = ([128, 128], U16)
+    SB["l2" + _s] = ([128, 128], U16)
+    SB["hi" + _s] = ([128, 128], BF)
+    SB["lo" + _s] = ([128, 128], BF)
+PS = ["key0", "key1", "pS", "pD1", "pD2", "pT1", "pT2", "pT3"]
+SCRATCH = {k: ("sbuf", v[0], v[1]) for k, v in SB.items()}
+for _p in PS:
+    SCRATCH[_p] = ("psum", [128, 512], F32)
+
+ENG = ["pe", "dve", "act", "pool", "sp"]
+XSEND = [(u, d) for u in range(R - 1) for d in (1, 2, 3) if any(t % 3 + 1 == d for t in range(u + 1, R))]
+SEMAPHORES = (["c_" + e for e in ENG[:4]] + ["d%d" % i for i in range(60)] + ["sent"] + ["xi%d" % d for d in (1, 2, 3)]
+              + ["al%d" % d for d in (1, 2, 3)] + ["dq%d" % t for t in range(R)] + ["xn%d_%d" % ud for ud in XSEND])
+
+CYC, GA, SC, PEC = 1.04, 1.56, 3.8, 0.52
+HOP = 150.0
+
+
+def build(T, topo, core, rank):
+    ops = []
+
+    def V(name, c0=None, c1=None, st=None, p=None):
+        ncol = 512 if name in PS else SB[name][0][1]
+        a = 0 if c0 is None else c0
+        b = ncol if c1 is None else c1
+        ps = slice(None) if p is None else slice(*p)
+        cs = slice(a, b) if st is None else slice(a, b, st)
+        n = len(range(a, b, st or 1))
+        w = 4 if name in PS else SZ[SB[name][1]]
+        return {"ap": T[name][ps, cs], "reg": [(name, a, b, st or 1)], "n": n, "w": w, "ps": name in PS}
+
+    def V4(name, idx, n):
+        return {"ap": T[name][idx], "reg": [(name, 0, 1 << 20)], "n": n, "w": SZ[SB[name][1]], "ps": False}
+
+    def IND(win, off):
+        return {"ap": win["ap"].indirect(off["ap"]), "reg": win["reg"] + off["reg"], "n": 16 * off["n"], "w": 4,
+                "ps": False, "ind": True, "off": off["reg"], "win": win["reg"]}
+
+    def ap(x):
+        return x["ap"] if isinstance(x, dict) else x
+
+    def regs(xs):
+        r = []
+        for x in xs:
+            if isinstance(x, dict):
+                r += x["reg"]
+        return r
+
+    def add(eng, fn, rd, wr, cost, **kw):
+        o = {"eng": eng, "fn": fn, "rd": rd, "wr": wr, "cost": cost, "id": len(ops)}
+        o.update(kw)
+        ops.append(o)
+        return o
+
+    def vcost(out, ins, two):
+        if out.get("ind"):
+            return 50 + out["n"] * SC * CYC
+        if ins[0].get("ind"):
+            return 50 + out["n"] * GA * CYC
+        f = 1.0
+        if two and not any(x["ps"] for x in ins):
+            f = 2.0
+        elif not two and out["w"] == 2 and all(x["w"] == 2 for x in ins):
+            f = 0.5
+        return 20 + max(64, out["n"] * f) * CYC
+
+    def vadd(fn, out, ins, extra, two):
+        rd = regs(ins + extra)
+        wr = out["reg"]
+        if out.get("ind"):
+            rd = rd + out["off"]
+            wr = out["win"]
+        return add("dve", fn, rd, wr, vcost(out, ins, two))
+
+    def cp(out, a):
+        vadd(lambda g: g.vector.tensor_copy(out["ap"], a["ap"]), out, [a], [], False)
+
+    setup = [False]
+
+    def ts(out, a, s1, o1, s2=None, o2=None):
+        if setup[0] and o2 is None and o1 == ALU.mult and a["n"] >= setup[0]:
+            act(out, a, AF.Copy, None, s1)
+        elif o2 is None:
+            vadd(lambda g: g.vector.tensor_scalar(out["ap"], a["ap"], ap(s1), None, o1), out, [a], [s1], False)
+        else:
+            vadd(lambda g: g.vector.tensor_scalar(out["ap"], a["ap"], ap(s1), ap(s2), o1, o2), out, [a], [s1, s2], False)
+
+    def tt(out, a, b, o):
+        vadd(lambda g: g.vector.tensor_tensor(out["ap"], a["ap"], b["ap"], o), out, [a, b], [], True)
+
+    def scan(out, d0, d1, o0, o1):
+        vadd(lambda g: g.vector.tensor_tensor_scan(out["ap"], d0["ap"], d1["ap"], 0.0, o0, o1), out, [d0, d1], [], False)
+
+    def ms(out, c):
+        vadd(lambda g: g.vector.memset(out["ap"], c), out, [out], [], False)
+
+    def act(out, a, func=AF.Copy, bias=None, scale=None):
+        kw = {}
+        if bias is not None:
+            kw["bias"] = ap(bias)
+        if scale is not None:
+            kw["scale"] = ap(scale)
+        c = 65 + out["n"] * (GA if a.get("ind") else 1.0) * CYC
+        add("act", lambda g: g.scalar.activation(out["ap"], a["ap"], func, **kw), regs([a, bias, scale]), out["reg"], c)
+
+    def mm(items):
+        def fn(g):
+            ins = None
+            for o, l, r, s0, s1 in items:
+                ins = g.tensor.matmul(o["ap"], l["ap"], r["ap"], s0, s1)
+            return ins
+        c = 30.0
+        rd, wr = [], []
+        for o, l, r, s0, s1 in items:
+            c += max(min(64, l["n"]), r["n"]) * (4 if r["w"] == 4 else 1) * PEC
+            rd += l["reg"] + r["reg"]
+            wr += o["reg"]
+        add("pe", fn, rd, wr, c)
+
+    def grp(out, pairs, first=True, last=True):
+        mm([(out, l, r, first and i == 0, last and i == len(pairs) - 1) for i, (l, r) in enumerate(pairs)])
+
+    def iota(out, pat, base=0, cm=0, fl=True):
+        kw = {"allow_small_or_imprecise_dtypes": True} if fl else {}
+        add("pool", lambda g: g.iota(out["ap"], pat, base, cm, **kw), [], out["reg"], 130 + 2 * CYC * out["n"])
+
+    def pcopy(out, a):
+        add("pool", lambda g: g.affine_select(out["ap"], a["ap"], [[0, out["n"]]], ALU.is_ge, 0.0, 1, 0),
+            a["reg"], out["reg"], 170 + 2 * CYC * out["n"])
+
+    nd = [0]
+
+    def dma(pairs, rd, wr, nbytes, q="sp"):
+        sem = "d%d" % nd[0]
+        nd[0] += 1
+
+        def fn(g):
+            e = g.sync if q == "sp" else g.scalar
+            for o, i in pairs:
+                e.dma_start(o, i).then_inc(T.sem[sem], 16)
+            return None
+        add(q, fn, rd, wr, 60.0 * len(pairs), lat=1800 + nbytes / 150.0, sem=sem, cnt=16 * len(pairs))
+
+    def send(dst_rank, out, a, sem, ne=16):
+        dst = T.cores[dst_rank % N]
+        rid, pid = topo.addr(dst)[:2]
+        mask = 0
+        for e in topo.engines(core, dst)[:ne]:
+            mask |= 1 << e
+        o = add("pool", lambda g: g.remote_dma(out["ap"], a["ap"], T.sem[sem], T.sem.sent, pid, rid, mask),
+                a["reg"], [], 400.0, rem=ne)
+        add("recv", None, [], out["reg"], 0.0, lat=2500 + 128 * a["n"] * a["w"] / 120.0, sem=sem, cnt=ne, after=o["id"])
+
+    yk, yx = T.yk, T.yx
+    col = lambda name, j: V(name, j, j + 1)
+
+    hb = B // 2
+    dma([(T.kint[:, 0:hb], T.kin[:, 0:hb])], [], [("kint", 0, hb)], 128 * hb * 4)
+    dma([(T.kint[:, hb:B], T.kin[:, hb:B])], [], [("kint", hb, B)], 128 * hb * 4, q="act")
+    dma([(T.X[:, 0:B], T.xf[:])], [], [("X", 0, B)], 128 * B * 2)
+    dma([(T.wI[:, 0:6], T.w[:]), (T.thI[0:1, 0:48], T.th[:])], [], [("wI", 0, 8), ("thI", 0, 48)], 4096)
+
+    iota(col("pI", 0), [[0, 1]], 0, 1, False)
+    iota(V("J"), [[1, 256]])
+    iota(V("JB"), [[0, 16], [1, 16]])
+    ts(col("pI", 1), col("pI", 0), 15, ALU.bitwise_and)
+    ts(col("pI", 2), col("pI", 0), 4, ALU.arith_shift_right)
+    cp(V("pF", 0, 3), V("pI", 0, 3))
+    pr, pg = col("pF", 1), col("pF", 2)
+    ts(col("pF", 3), col("pF", 0), 16.0, ALU.add)
+    ts(V("IW"), V("J", 0, 176), col("pF", 3), ALU.is_equal)
+    ts(V("RM"), V("J", 0, 16), pr, ALU.is_equal)
+    I32v = V("IW", 16, 144)
+    ts(col("pF", 4), pr, 9.0, ALU.is_ge)
+    ts(col("pF", 5), pr, 8.0, ALU.is_ge)
+    ts(col("pF", 6), pr, 8.0, ALU.is_lt)
+    tt(col("pF", 7), col("pF", 4), col("RM", 0), ALU.add)
+    ts(col("pF", 7), col("pF", 7), -1.0, ALU.mult, 1.0, ALU.add)
+    tt(col("pF", 8), col("RM", 6), col("RM", 7), ALU.add)
+    ts(col("pF", 9), col("pF", 8), -1.0, ALU.mult, 1.0, ALU.add)
+    ts(col("pF", 10), pr, 6.0, ALU.is_le, BIG, ALU.mult)
+    setup[0] = 8 if ACT16 else False
+    ts(V("tmpc", 0, 176), V("IW"), col("pF", 4), ALU.mult)
+    ts(V("MC"), V("IW"), col("RM", 0), ALU.mult)
+    for h in range(2):
+        tt(V("MB", 128 * h, 128 * h + 128), V("tmpc", 25 - 8 * h, 153 - 8 * h), V("MC", 9 - 8 * h, 137 - 8 * h), ALU.add)
+    ts(V("MA"), V("IW"), col("pF", 7), ALU.mult)
+    for r in range(16):
+        if not ACT16:
+            act(V("W32", 144 * r, 144 * r + 144), V("IW", r + 1, r + 145), AF.Copy, None, col("RM", r))
+        ts(V("W16", 144 * r, 144 * r + 144), V("IW", r + 1, r + 145), col("RM", r), ALU.mult)
+    w32 = lambda r, b: V("W32", 144 * r + 15 - b, 144 * r + 143 - b)
+    w16 = lambda r, b: V("W16", 144 * r + 15 - b, 144 * r + 143 - b)
+    iota(V("KB", 0, B), [[0, B // 8], [1, 8]])
+    ops[-1]["rd"] = [("JB", 0, 256), ("J", 0, 256)]
+    cp(V("K0", 0, hb), V("kint", 0, hb))
+    cp(V("K0", hb, B), V("kint", hb, B))
+
+    def kbcopy(src, c0, c1):
+        dma([(T.KB[16 * g:16 * g + 6, c0:c1], T[src][16 * g:16 * g + 6, c0:c1]) for g in range(8)],
+            [(src, c0, c1)], [("KB", c0, c1)], 48 * (c1 - c0) * 4)
+    kbcopy("K0", 0, B)
+    dma([(T.K[:, 0:B], T.K0[:])], [("K0", 0, B), ("KB", 0, B)], [("K", 0, B)], 128 * B * 4)
+    ts(V("Blk", 0, 8), V("J", 0, 8), pg, ALU.is_equal)
+    ts(V("Blk", 8, 16), V("J", 0, 8), pg, ALU.is_gt)
+    blk, slt = V("Blk", 0, 8), V("Blk", 8, 16)
+    cp(V("Blk16"), blk)
+    act(V("Ib"), I32v)
+    act(V("nIb"), I32v, AF.Copy, None, -1.0)
+    act(V("hIb"), I32v, AF.Copy, None, 0.5)
+    for h in range(2):
+        for wi in range(2):
+            q = 2 * h + wi
+            ts(V("QW", 176 * q, 176 * q + 176), V("IW"), col("pF", 6 - h), ALU.mult, (0.0625, 1.0)[wi], ALU.mult)
+    for wi in range(2):
+        ts(V("RR", 8 * wi, 8 * wi + 8), blk, 4096.0, ALU.mult)
+        ts(V("RR", 16 + 8 * wi, 24 + 8 * wi), blk, col("pF", 10), ALU.mult)
+        ts(V("RR", 32 + 8 * wi, 40 + 8 * wi), blk, -4096.0, ALU.mult)
+    ts(V("RR", 48, 56), blk, 16.0, ALU.mult)
+    cp(V("repl"), V("J", 0, 16))
+    one = (0, 1)
+    for h in range(2):
+        iota(V("tmpc", 256 * h, 256 * h + 256, p=one), [[-120, 2], [0, 8], [256, 16]], 256 * 9 + 128)
+    ts(V("scn", 0, 256, p=one), V("JB", p=one), 7.0, ALU.is_ge, -4096.0, ALU.mult)
+    for h in range(2):
+        tt(V("kc", 256 * h, 256 * h + 256, p=one), V("tmpc", 256 * h, 256 * h + 256, p=one), V("scn", 0, 256, p=one), ALU.add)
+    ms(V("one16", p=one), 1.0)
+    for s in "SD":
+        if "d" in ROUTE[s]:
+            for c in range(4):
+                if ROUTE[s][c] != "d":
+                    ms(V("Dsg" + s, 512 * c, 512 * c + 512), 0.0)
+    for d in (1, 2, 3):
+        send(rank - d, V("XQ%d" % d, 0, B), V("X", 0, B), "xi%d" % d)
+        ops[-2]["rd"] = ops[-2]["rd"] + [("KB", 0, B)]
+    iota(V("KB", B, W), [[0, (W - B) // 8], [1, 8]])
+
+    def late_constants():
+        act(V("IH"), I32v)
+        cp(V("RR", 56, 64), blk)
+        ms(V("oneb"), 1.0)
+        ts(V("Dm"), V("JB"), pr, ALU.is_equal)
+        ts(V("wt"), V("JB"), pr, ALU.is_gt)
+        act(V("tmpc", 0, 256), V("Dm"), AF.Copy, None, EW)
+        tt(V("wt"), V("wt"), V("tmpc", 0, 256), ALU.add)
+        ts(V("Mm"), V("JB"), pr, ALU.is_le, 8192.0, ALU.mult)
+        for h in range(2):
+            ts(V("rst", 256 * h, 256 * h + 256), V("JB"), 0.0, ALU.is_equal, 1e9, ALU.mult)
+        ms(V("RE"), 0.0)
+        for ri, wv in enumerate((1.0 / 4096, 1.0, -1.0)):
+            for h in range(2):
+                c = 16 * ri + 8 * h
+                ts(V("RE", 48 * h + c, 48 * h + c + 8), blk, wv, ALU.mult)
+                ts(V("RE", 96 + 48 * h + c, 96 + 48 * h + c + 8), slt, wv, ALU.mult)
+            ms(V("RE", 96 + 16 * ri + 8, 96 + 16 * ri + 16), wv)
+        ts(V("CE", 48, 64), V("J", 0, 16), 16.0, ALU.mult, pr, ALU.add)
+        ts(V("CE", 0, 16), V("CE", 48, 64), 3.0, ALU.mult, -(0.5 - 1.0 / 8192), ALU.add)
+        ms(V("CE", 16, 32), 0.0)
+        ts(V("CE", 32, 48), V("CE", 48, 64), 256.0, ALU.add)
+        ts(V("CE", 48, 64), V("CE", 48, 64), 16.0, ALU.mult)
+        cp(V("J16"), V("J"))
+        cp(V("kca", p=one), V("JB", 0, 128, p=one))
+        ms(V("qc", p=one), -0.25)
+        cm = lambda j: V("CM", 128 * j, 128 * j + 128)
+        tt(cm(0), w16(0, 2), w16(1, 3), ALU.add)
+        tt(cm(0), cm(0), w16(7, 8), ALU.add)
+        ts(cm(1), I32v, col("pF", 4), ALU.mult)
+        tt(cm(1), cm(1), w16(0, 4), ALU.add)
+        tt(cm(1), cm(1), w16(1, 5), ALU.add)
+        ts(col("pF", 11), col("RM", 0), 8.0, ALU.mult, col("pF", 8), ALU.add)
+        ts(cm(2), I32v, col("pF", 11), ALU.mult)
+        ts(cm(3), I32v, col("pF", 9), ALU.mult)
+        ts(col("pF", 12), col("RM", 6), 8.0, ALU.mult, col("RM", 7), ALU.add)
+        ts(cm(4), I32v, col("pF", 12), ALU.mult)
+        for t in range(R):
+            tt(V("CA", 128 * t, 128 * t + 128), I32v, w16(9 + t, 9 + t), ALU.subtract)
+        j6 = V("J", 0, 6)
+        for kind, (mv, mn) in enumerate(((col("RM", 0), col("pF", 8)), (None, col("RM", 7)), (col("RM", 6), col("RM", 7)))):
+            ts(col("pF", 13), mn, 256.0, ALU.mult)
+            ts(col("pF", 14), col("pF", 13), 2048.0, ALU.add)
+            if mv is not None:
+                tt(col("pF", 13), col("pF", 13), mv, ALU.add)
+                ts(col("pF", 14), mv, -2048.0, ALU.mult, col("pF", 14), ALU.add)
+            ts(V("BI", 8 * kind, 8 * kind + 6), j6, col("pF", 13), ALU.mult, col("pF", 14), ALU.add)
+        ts(V("BI", 24, 30), j6, 256.0, ALU.mult, 256.0, ALU.add)
+        tt(V("BI", 24, 30), V("BI", 24, 30), V("RM", 9, 15), ALU.mult)
+        ts(V("BI", 24, 30), V("BI", 24, 30), 2048.0, ALU.add)
+        for q in range(4):
+            ms(V("E", 1024 * q, 1024 * q + 1024), 0.0)
+        ms(V("pc"), 0.0)
+        iota(V("tmpc", 256, 384), [[1, 8], [0, 16]])
+        ts(V("nBR"), V("tmpc", 256, 384), pg, ALU.is_equal, -1.0, ALU.mult)
+        ms(V("bJ"), 0)
+        setup[0] = False
+        ts(V("thF", p=one), V("thI", p=one), 4096.0, ALU.mult)
+        add("pool", lambda g: g.partition_broadcast(T.thB[:], T.thF[0:1, :], 128), [("thF", 0, 48)], [("thB", 0, 48)], 400.0)
+        for h in range(2):
+            cp(V("thz", 8 * h, 8 * h + 8), V("thB", 0, 48, 6))
+        cp(V("wF", 0, 6), V("wI", 0, 6))
+        for t in range(R):
+            ts(V("wS", 8 * t, 8 * t + 8), blk, col("wF", t), ALU.mult)
+        mm([(V("pT3", 16 * t + 8 * h, 16 * t + 8 * h + 8), xv(t, h), V("wS", 8 * t, 8 * t + 8), True, True)
+            for t in range(R) for h in range(2)])
+        cp(V("aI"), V("pT3", 0, 96))
+        ts(V("aJ"), V("aI"), 2047, ALU.bitwise_and)
+        asklists(1)
+
+    def asklists(d):
+        for j in range(2):
+            t = d - 1 + 3 * j
+            tt(V("aL"), IND(V("aJ", 16 * t, 16 * t + 16), V("repl")), V("Dm"), ALU.mult)
+            mm([(V("pT3", 128 + 16 * j + 8 * h, 136 + 16 * j + 8 * h), V("aL", 128 * h, 128 * h + 128), V("Blk16"), True, True)
+                for h in range(2)])
+        cp(V("aU", 32 * d - 32, 32 * d), V("pT3", 128, 160))
+        send(rank + d, V("aR", 32 * d - 32, 32 * d), V("aU", 32 * d - 32, 32 * d), "al%d" % d, 4)
+
+    def lanes(name, t, h=None):
+        if h is None:
+            return V(name, t, 2048, 8)
+        return V(name, t + 1024 * h, 1024 * h + 1024, 8)
+
+    def xv(t, h=None):
+        return lanes("X", t, h)
+
+    def spread(name, src, t):
+        for b in range(16):
+            if t == 0 and (b % 3 == 0 or src == "X" and b % 3 == 1):
+                act(V(name, b, 2048, 16), lanes(src, t, b // 8))
+            elif t == 0 and (b % 3 == 1 or src == "X"):
+                cp(V(name, b, 2048, 16), lanes(src, t, b // 8))
+            else:
+                pcopy(V(name, b, 2048, 16), lanes(src, t, b // 8))
+
+    def batch(t, s):
+        a = slice(None)
+        cnt = B + L * t
+        still = s == "S" or t == 0
+        kt, wn = ("K0", B) if still else ("K", cnt)
+        key = "key%d" % (t % 2)
+        pe = "pS" if s == "S" else "pD1"
+        slot0 = 0 if s == "S" else 8
+        ks = [(slot0 + kk + 9) % 16 for kk in range(8)]
+        if s == "S":
+            mm([(V(key), V("one16", p=one), V("kc", p=one), True, False)])
+            grp(V(pe, 0, 128), [(V("MB", 128 * h, 128 * h + 128), lanes(kt, t, h)) for h in range(2)])
+            cp(V("l1" + s), V(pe, 0, 128))
+        else:
+            ts(V("kv16"), lanes(kt, t), -2048.0, ALU.add)
+            grp(V(pe, 0, 128), [(V("MA", 17 - 8 * h, 145 - 8 * h), V("kv16", 128 * h, 128 * h + 128)) for h in range(2)])
+            ts(V("l1" + s), V(pe, 0, 128), 2048.0, ALU.add)
+        for hf in range(2):
+            dv = hf < ADVE[s]
+            half = dv or ACT16
+            gb = ("G16" if half else "G32") + s
+            for c in (2 * hf, 2 * hf + 1):
+                src = IND(V(kt, 0, wn), V("l1" + s, 32 * c, 32 * c + 32))
+                if dv:
+                    ts(V(gb, 512 * c, 512 * c + 512), src, -2048.0, ALU.add)
+                else:
+                    act(V(gb, 512 * c, 512 * c + 512), src, AF.Copy, -2048.0)
+            st = 8 if half else 4
+            for b0 in range(0, 16, st):
+                grp(V(pe, 128 + 64 * hf, 192 + 64 * hf),
+                    [((w16 if half else w32)((ks[b % 8] + t) % 16, b), V(gb, 1024 * hf + b, 1024 * hf + 1024, 16))
+                     for b in range(b0, b0 + st)], b0 == 0, b0 + st == 16)
+        cP = V(pe, 128, 256)
+        ts(V("l2" + s), cP, 2048.0, ALU.add)
+        ts(V("hi" + s), cP, 16 * MAG0, ALU.add, 16 * MAG0, ALU.subtract)
+        tt(V("lo" + s), cP, V("hi" + s), ALU.subtract)
+        mm([(V(key, 256 * h + 128 * wi, 256 * h + 128 * wi + 128), V(("hi", "lo")[wi] + s),
+             V("QW", 176 * (2 * h + wi) + 16 - slot0 + 8 * h, 176 * (2 * h + wi) + 144 - slot0 + 8 * h), False, False)
+            for h in range(2) for wi in range(2)])
+        kvb, xvb = "kvb%d" % (t % 2), "xvb%d" % (t % 2)
+        for c in range(4):
+            off = V("l2" + s, 32 * c, 32 * c + 32)
+            cs = (512 * c, 512 * c + 512)
+            rt = ROUTE[s][c]
+            if rt == "a":
+                bank = "pS" if s == "S" else ("pD2", "pD1")[c % 2]
+                act(V("Xc" + s, *cs), IND(V("X", 0, wn), off))
+                grp(V(bank), [(V("Ib"), V("Xc" + s, *cs)), (V("nIb"), V(xvb, *cs))])
+                act(V("Dab" + s, *cs), V(bank), AF.Abs)
+            elif rt == "b":
+                tt(V("Xc" + s, *cs), IND(V("X", 0, wn), off), V(xvb, *cs), ALU.subtract)
+                act(V("Dab" + s, *cs), V("Xc" + s, *cs), AF.Abs)
+            else:
+                tt(V("Dsg" + s, *cs), IND(V("X", 0, wn), off), V(xvb, *cs), ALU.subtract)
+                ts(V("Dab" + s, *cs), V("Dsg" + s, *cs), 0.0, ALU.max, 2.0, ALU.mult)
+            tt(V("eq" + s, *cs), IND(V("KB", 0, wn), off), V(kvb, *cs), ALU.is_equal)
+        ko = lambda b: V(key, 256 * (b // 8) + slot0 + b % 8, 256 * (b // 8) + 256, 16)
+        for b0 in range(0, 16, 8):
+            mm([(ko(b), V("eq" + s, b, 2048, 16), V("RR", 16, 32), False, False) for b in range(b0, b0 + 8)])
+        if "d" in ROUTE[s]:
+            for b0 in range(0, 16, 8):
+                mm([(ko(b), V("Dsg" + s, b, 2048, 16), V("RR", 32, 48), False, False) for b in range(b0, b0 + 8)])
+        for b0 in range(0, 16, 8):
+            mm([(ko(b), V("Dab" + s, b, 2048, 16), V("RR", 0, 16), False, s == "D" and b == 15) for b in range(b0, b0 + 8)])
+
+    def tail(t):
+        cnt = B + L * t
+        kt = "K0" if t == 0 else "K"
+        key = "key%d" % (t % 2)
+        d = t % 3 + 1
+        cm = lambda j: V("CM", 128 * j, 128 * j + 128)
+        sm = lambda j: V("sm", 16 * j, 16 * j + 16)
+        ul = lambda j: V("uL", 16 * j, 16 * j + 16)
+        rep = V("repl")
+        ac = 32 * d - 32 + 16 * (t // 3)
+        act(V("dS", L * t, L * t + L), IND(V(kt, 0, 2048), V("aR", ac, ac + 16)), AF.Copy, None, 512.0)
+        send(rank - d, V("dR", L * t, L * t + L), V("dS", L * t, L * t + L), "dq%d" % t, 8)
+        if t < 2:
+            asklists(t + 2)
+        kv = lanes(kt, t)
+        pcopy(V("pk"), xv(t))
+        for nm, j in (("KW", 1), ("KW", 2), ("SW", 2)):
+            pcopy(V(nm, j, 768, 3), kv)
+        for j in (1, 2):
+            pcopy(V("XW", j, 768, 3), xv(t))
+        grp(V("pT3", 0, 256), [(V("CA", 128 * t, 128 * t + 128), V("kv16")), (w16(9 + t, 9 + t), V("J16"))])
+        act(V("SW", 1, 768, 3), V("pT3", 0, 256), AF.Identity, col("BI", 24 + t))
+        scan(V("scn"), V("rst"), V(key), ALU.add, ALU.min)
+        cp(V("kI"), V("scn", 15, 512, 16))
+        ts(V("kJ"), V("kI"), 0x7F0000FF, ALU.bitwise_and)
+        for h in range(2):
+            ts(V("sm", 8 * h, 8 * h + 8), V("kJ", 16 * h, 16 * h + 8), 16.0, ALU.mult, 6144.0, ALU.min)
+            ts(V("sm", 16 + 8 * h, 24 + 8 * h), V("kJ", 16 * h + 8, 16 * h + 16), 255.0, ALU.min, -2056.0, ALU.add)
+        tt(V("mT"), sm(0), sm(1), ALU.add)
+        tt(V("LM"), IND(V("mT"), rep), V("Dm"), ALU.mult)
+        act(V("LR"), IND(V("mT"), rep))
+        for h in range(2):
+            tt(V("nk", 8 * h, 8 * h + 8), V("scn", 256 * h + 15, 256 * h + 128, 16), V("thz", 8 * h, 8 * h + 8), ALU.is_lt)
+        mm([(V("pT3", 256 + 8 * h, 264 + 8 * h), V("LM", 128 * h, 128 * h + 128), V("Blk16"), True, True) for h in range(2)])
+        mm([(V("pT1", 128 * h, 128 * h + 128), V("LR", 128 * h, 128 * h + 128), V("IH"), True, True) for h in range(2)])
+        mWp = V("pT3", 256, 272)
+        cp(V("mW"), mWp)
+        ts(ul(0), mWp, 2048.0, ALU.add, float(cnt - 1), ALU.min)
+        ts(sm(2), mWp, float(cnt - 1 - 2048), ALU.min, 2048.0 + EW - cnt, ALU.add)
+        cp(V("mR"), V("pT1", 0, 256))
+        mm([(V("pD2", 0, 256), V("Ib"), V("Mm"), True, False)]
+           + [(V("pD2", 128 * h, 128 * h + 128), V(nm, 128 * h, 128 * h + 128), V(rh), False, nm == "LM" and h == 1)
+              for nm, rh in (("LR", "IH"), ("LM", "nBR")) for h in range(2)])
+        act(V("xm"), IND(V("X", 0, cnt), ul(0)))
+        cP = lambda h: V("pT2", 8 * h, 8 * h + 8)
+        Eh = lambda s, h: V("E", 256 * s + 128 * h, 256 * s + 128 * h + 128)
+        b1 = V("RR", 56, 64)
+        mm([(V("pT2", 0, 16), V("nIb"), V("nk"), True, False)])
+        for s in range(15):
+            ts(V("E", 256 * s + 16 * s + 16, 256 * s + 256), V("mR", 16 * s + 16, 256), col("mW", s), ALU.is_equal)
+            if s % 3 == 2:
+                mm([(cP(h), Eh(u, h), b1, False, False) for u in range(s - 2, s + 1) for h in range(2) if h == 1 or u < 7])
+        ts(V("E", 256 * 15, 256 * 16), V("pD2", 0, 256), 0.0, ALU.is_equal)
+        mm([(cP(h), Eh(15, h), b1, False, h == 1) for h in range(2)])
+        if ACT16:
+            act(V("km16"), IND(V(kt, 0, cnt), ul(0)), AF.Copy, -2048.0)
+        else:
+            ts(V("km16"), IND(V(kt, 0, cnt), ul(0)), -2048.0, ALU.add)
+        eP = V("pT1", 256, 304)
+        mm([(eP, I32v, V("CE", 0, 48), True, False)])
+        ts(V("lost"), V("pT2", 0, 16), 0.0, ALU.is_ge)
+        tt(V("Lw"), IND(V("lost"), rep), V("wt"), ALU.mult)
+        act(V("Lr"), IND(V("lost"), rep))
+        grp(eP, [(V(nm, 128 * h, 128 * h + 128), V("RE", o + 48 * h, o + 48 * h + 48))
+                 for nm, o in (("Lw", 0), ("Lr", 96)) for h in range(2)], False, True)
+        grp(V("pD2", 0, 256), [(cm(3), V("kv16")), (w16(7, 7), V("J16")), (w16(6, 6), V("mR"))])
+        act(V("SW", 0, 768, 3), V("pD2", 0, 256), AF.Identity, col("BI", 8 + t))
+        grp(V("pD1", 0, 256), [(cm(4), V("J16")), (cm(3), V("km16"))])
+        act(V("kmN"), V("pD1", 0, 256), AF.Identity, col("BI", 16 + t))
+        grp(V("pD2", 256, 512), [(cm(0), V("kv16")), (cm(2), V("J16")), (w16(1, 1), V("mR")), (cm(1), V("km16"))])
+        act(V("KW", 0, 768, 3), V("pD2", 256, 512), AF.Identity, col("BI", t))
+        grp(V("pT3", 0, 256), [(V("oneb", p=one), V("qc", p=one)), (V("hIb"), xv(t)), (V("hIb"), V("xm"))])
+        ts(V("XW", 0, 768, 3), V("pT3", 0, 256), MAG0, ALU.add, MAG0, ALU.subtract)
+        ts(ul(1), V("pT1", 256, 272), MAG0, ALU.add, MAG0, ALU.subtract)
+        tt(sm(3), V("pT1", 272, 288), sm(2), ALU.max)
+        ts(sm(4), V("pT1", 272, 288), -EW, ALU.add)
+        ts(ul(2), sm(3), cnt - EW, ALU.add)
+        tt(sm(5), V("pT1", 288, 304), sm(4), ALU.max)
+        ts(sm(6), V("pT1", 256, 272), MAG0, ALU.add, MAG0, ALU.subtract)
+        cp(ul(3), sm(5))
+        cp(IND(V("K", 0, cnt + L), ul(2)), V("kmN"))
+        act(lanes("K", t), IND(V("SW"), ul(1)))
+        act(V("K", cnt, cnt + L), IND(V("KW"), ul(1)))
+        if t < R - 1:
+            kbcopy("K", cnt, cnt + L)
+        tt(IND(V("pc"), ul(3)), V("dR", L * t, L * t + L), V("pk"), ALU.add)
+        ts(V("dU"), V("pc", 0, 64), 1.0 / 512, ALU.mult)
+        ts(V("pr"), V("pc", 0, 64), 512 * MAG0, ALU.add, 512 * MAG0, ALU.subtract)
+        tt(V("xc"), V("pc", 0, 64), V("pr"), ALU.subtract)
+        for c in range(2):
+            (cp if c == 1 and t == R - 1 else act)(V("Xa", 512 * c, 512 * c + 512),
+                                                   IND(V("XQ%d" % d, 0, cnt), V("dU", 32 * c, 32 * c + 32)))
+        lo = (0, 64)
+        mm([(V("pT2", 0, 128, p=lo), V("one16", 0, 64, p=one), V("kca", p=one), True, False)])
+        for c in range(2):
+            bank = ("pT3", "pT1")[c]
+            mm([x for k in range(8 * c, 8 * c + 8) for x in
+                ((V(bank, 64 * (k % 8), 64 * (k % 8) + 64), V("Ib"), V("Xa", k, 1024, 16), True, False),
+                 (V(bank, 64 * (k % 8), 64 * (k % 8) + 64), V("nIb"), V("xc"), False, True))])
+            act(V("Da", 512 * c, 512 * c + 512), V(bank), AF.Abs)
+            mm([(V("pT2", k, 128, 16, p=lo), V("Da", 64 * k, 64 * k + 64), V("RR", 48, 56), False, k == 15)
+                for k in range(8 * c, 8 * c + 8)])
+        ts(sm(7), sm(4), 768.0, ALU.add)
+        ts(sm(8), sm(4), 64.0, ALU.is_lt, 4096.0, ALU.mult)
+        tt(sm(7), sm(7), sm(8), ALU.min)
+        tt(sm(7), sm(7), sm(6), ALU.max)
+        cp(ul(4), sm(7))
+        scan(V("asn", p=lo), V("rst", 0, 128, p=lo), V("pT2", 0, 128, p=lo), ALU.add, ALU.min)
+        cp(V("bI", p=lo), V("asn", 15, 128, 16, p=lo))
+        ts(V("bJ", p=lo), V("bI", p=lo), 15, ALU.bitwise_and)
+        tt(V("bL"), IND(V("bJ"), V("repl", 0, 8)), V("Dm", 0, 128), ALU.mult)
+        grp(V("pT2", 256, 260), [(I32v, V("CE", 48, 52)), (V("bL", p=lo), V("Blk16", 0, 4, p=lo))])
+        cp(V("uL", 80, 84), V("pT2", 256, 260))
+        act(V("XW", 768, 832), IND(V("Xa"), V("uL", 80, 84)))
+        act(V("X", cnt, cnt + L), IND(V("XW"), ul(4)))
+        for u, dd in sorted(XSEND, key=lambda x: (x[1] - (t + 1) % 3 - 1) % 3):
+            if u == t:
+                send(rank - dd, V("XQ%d" % dd, cnt, cnt + L), V("X", cnt, cnt + L), "xn%d_%d" % (u, dd), 8)
+        if t < R - 1:
+            grp(V("pT3", 0, 16), [(V("oneb"), V("Lr", 0, 256, 16))])
+            add("dve", lambda g: g.vector.tensor_reduce(T.zF[:, 0:1], T.pT3[:, 0:16], AX.X, ALU.add),
+                [("pT3", 0, 16)], [("zF", 0, 1)], 90.0)
+            ts(col("zI", 0), col("zF", 0), -1.0, ALU.mult, 2048.0, ALU.add)
+            ts(col("zI", 1), col("zI", 0), 15, ALU.bitwise_and)
+            ts(col("zF", 1), col("zI", 1), 4096.0, ALU.mult)
+            for h in range(2):
+                ts(V("thz", 8 * h, 8 * h + 8), V("thB", t + 1, 48, 6), col("zF", 1), ALU.add, BIG, ALU.min)
+        pairs = [(yk[:, cnt:cnt + L], T.K[:, cnt:cnt + L]), (yk[9 + t:128:16, 0:2048], T.K[9 + t:128:16, 0:2048])]
+        nb = 128 * 1024 + 65536
+        if t == R - 1:
+            pairs += [(yk[r:128:16, 0:cnt], T.K[r:128:16, 0:cnt]) for r in (6, 7)]
+            nb += 16 * cnt * 4
+        dma(pairs, [("K", 0, cnt + L)], [("yk", 0, W)], nb)
+        dma([(yx[:, L * t:L * t + L], T.X[:, cnt:cnt + L])], [("X", cnt, cnt + L)], [("yx", L * t, L * t + L)], 65536)
+
+    spread("kvb0", "KB", 0)
+    spread("xvb0", "X", 0)
+    batch(0, "S")
+    late_constants()
+    for t in range(R):
+        batch(t, "D")
+        if t == 0:
+            dma([(yk[:, 0:B], T.K0[:])], [("K0", 0, B), ("eqD", 0, 512)], [("yk", 0, W)], 128 * B * 4)
+        if t + 1 < R:
+            spread("kvb%d" % ((t + 1) % 2), "KB", t + 1)
+            spread("xvb%d" % ((t + 1) % 2), "X", t + 1)
+            batch(t + 1, "S")
+        tail(t)
+    return ops
+
+
+def depend(ops):
+    hist = {}
+    for o in ops:
+        dep = {}
+        if "after" in o:
+            dep[o["after"]] = True
+        acc = [(r, False) for r in o["rd"]] + [(r, True) for r in o["wr"]]
+        acc = [(r[0], r[1], r[2], r[3] if len(r) > 3 else 1, w) for r, w in acc]
+        for name, a, b, st, w in acc:
+            for (a2, b2, w2, j, st2) in hist.get(name, []):
+                if j == o["id"]:
+                    continue
+                if name in PS:
+                    dep[j] = dep.get(j, False) or ops[j]["eng"] != o["eng"]
+                elif (w or w2) and a < b2 and a2 < b and (st != st2 or (a - a2) % st == 0):
+                    dep[j] = True
+        for name, a, b, st, w in acc:
+            hs = hist.setdefault(name, [])
+            if name in PS:
+                if any(ops[x[3]]["eng"] != o["eng"] for x in hs):
+                    hs[:] = [x for x in hs if x[3] == o["id"]]
+            elif w and st == 1:
+                hs[:] = [x for x in hs if not (a <= x[0] and x[1] <= b) or x[3] == o["id"]]
+            hs.append((a, b, w, o["id"], st))
+        o["dep"] = dep
+
+
+def schedule(ops):
+    n = len(ops)
+    succ = [[] for _ in range(n)]
+    for o in ops:
+        for j in o["dep"]:
+            succ[j].append(o["id"])
+    dur = [o["cost"] + o.get("lat", 0.0) for o in ops]
+    prio = [0.0] * n
+    for i in range(n - 1, -1, -1):
+        prio[i] = dur[i] + max([prio[k] + (HOP if ops[k]["dep"][i] else 0.0) for k in succ[i]] + [0.0])
+    left = [len(o["dep"]) for o in ops]
+    ready = [i for i in range(n) if left[i] == 0]
+    rdy = [0.0] * n
+    free = {}
+    order = []
+    while ready:
+        est = {i: max(rdy[i], free.get(ops[i]["eng"], 0.0)) for i in ready}
+        i0 = min(ready, key=lambda i: (est[i], -prio[i]))
+        e = ops[i0]["eng"]
+        pick = i0
+        if e != "recv":
+            for i in ready:
+                if ops[i]["eng"] == e and prio[i] > prio[pick] and est[i] < est[i0] + 0.5 * ops[i0]["cost"]:
+                    pick = i
+        o = ops[pick]
+        o["t0"] = est[pick]
+        if e != "recv":
+            free[e] = est[pick] + o["cost"]
+        o["t1"] = est[pick] + dur[pick]
+        order.append(pick)
+        ready.remove(pick)
+        for k in succ[pick]:
+            rdy[k] = max(rdy[k], o["t1"] + (HOP if ops[k]["dep"][pick] else 0.0))
+            left[k] -= 1
+            if left[k] == 0:
+                ready.append(k)
+    return order
+
+
+def place(ops, seq, pred, back):
+    t0 = [0.0] * len(ops)
+    gaps = {e: [[0.0, 1e12]] for e in ENG}
+    end = 0.0
+    for i in seq:
+        o = ops[i]
+        c, lat = o["cost"], o.get("lat", 0.0)
+        r = lat if back else 0.0
+        for j, hard in pred[i]:
+            x = t0[j] + ops[j]["cost"]
+            if hard:
+                x += HOP + (lat if back else ops[j].get("lat", 0.0))
+            r = max(r, x)
+        if o["eng"] != "recv":
+            gl = gaps[o["eng"]]
+            k = len(gl) - 1
+            while k > 0 and gl[k - 1][1] >= r + c:
+                k -= 1
+            while max(gl[k][0], r) + c > gl[k][1]:
+                k += 1
+            a, b = gl[k]
+            r = max(a, r)
+            gl[k:k + 1] = [x for x in ([a, r], [r + c, b]) if x[1] - x[0] > 40.0 or x[1] > 1e11]
+        t0[i] = r
+        end = max(end, r + c + (0.0 if back else lat))
+    return t0, end
+
+
+SHAKE = 3000.0
+
+
+def improve(ops, rounds=400):
+    n = len(ops)
+    pred = [list(o["dep"].items()) for o in ops]
+    succ = [[] for _ in range(n)]
+    for o in ops:
+        for j, hard in o["dep"].items():
+            succ[j].append((o["id"], hard))
+    seq = schedule(ops)
+    best = None
+    x = [12345]
+
+    def rnd():
+        x[0] = (x[0] * 1103515245 + 12345) % 2147483648
+        return x[0] / 2147483648.0
+    for it in range(rounds):
+        t0, end = place(ops, seq, pred, False)
+        if best is None or end < best[0]:
+            best = (end, t0)
+        if it % 4 == 3:
+            lo = rnd() * best[0]
+            key = [0.0] * n
+            for i in range(n):
+                k = best[1][i]
+                if lo <= k < lo + 30000.0:
+                    k += (rnd() - 0.5) * SHAKE
+                key[i] = max([k] + [key[j] + 1e-3 for j, _h in pred[i]])
+            seq = sorted(range(n), key=lambda i: (key[i], i))
+            continue
+        seq = sorted(range(n), key=lambda i: (-(t0[i] + ops[i]["cost"] + ops[i].get("lat", 0.0)), -i))
+        tb, _e = place(ops, seq, succ, True)
+        seq = sorted(range(n), key=lambda i: (-(tb[i] + ops[i]["cost"]), i))
+    for o in ops:
+        o["t0"] = best[1][o["id"]]
+        o["t1"] = o["t0"] + o["cost"] + o.get("lat", 0.0)
+    return sorted(range(n), key=lambda i: (best[1][i], i))
+
+
+ORDER = {}
+
+
+def rank_program(g, core, T, topo):
+    rank = T.rank_of(core)
+    if rank is None:
+        return
+    ops = build(T, topo, core, rank)
+    depend(ops)
+    if "all" not in ORDER:
+        ORDER["all"] = improve(ops)
+    order = ORDER["all"]
+    queue = {"pe": g.tensor, "dve": g.vector, "act": g.scalar, "pool": g, "sp": g.sync}
+    needed = set(j for o in ops for j, hard in o["dep"].items() if hard)
+    count = {e: 0 for e in ENG}
+    mark = {}
+    seen = {e: {} for e in ENG}
+    sent = 0
+    for i in order:
+        o = ops[i]
+        e = o["eng"]
+        if e == "recv":
+            mark[i] = (o["sem"], o["cnt"])
+            continue
+        want = {}
+        for j, hard in o["dep"].items():
+            if hard and j in mark:
+                s, v = mark[j]
+                want[s] = max(want.get(s, 0), v)
+        for s, v in want.items():
+            if seen[e].get(s, 0) < v:
+                queue[e].wait_ge(T.sem[s], v)
+                seen[e][s] = v
+        ins = o["fn"](g)
+        if "sem" in o:
+            mark[i] = (o["sem"], o["cnt"])
+        elif "rem" in o:
+            sent += o["rem"]
+        elif i in needed:
+            count[e] += 1
+            ins.then_inc(T.sem["c_" + e], 1)
+            mark[i] = ("c_" + e, count[e])
+    final = {}
+    for s, v in mark.values():
+        final[s] = max(final.get(s, 0), v)
+    final["sent"] = sent
+    for s, v in final.items():
+        if max(seen[e].get(s, 0) for e in ENG) < v:
+            g.sync.wait_ge(T.sem[s], v)

@@ -1,3 +1,4 @@
+from concourse.bass import DstId, RemoteDMATransfer
 from concourse.mybir import AluOpType as ALU, AxisListType as AX, ActivationFunctionType as AF
 
 N, R, L, B, W = 4, 6, 256, 2304, 3840
@@ -5,64 +6,78 @@ F32, BF, F16, I32, U16 = "float32", "bfloat16", "float16", "int32", "uint16"
 SZ = {F32: 4, BF: 2, F16: 2, I32: 4, U16: 2}
 EW = 8128.0
 MAG0 = 12582912.0
-BIG = 16777216.0
+BIG = 33554432.0
+MID = 1920
+PAD = 256
 
-ROUTE = {"S": "aaaa", "D": "aaad"}
-ACT16 = True
-HF = F16 if ACT16 else F32
-ADVE = {"S": 0, "D": 1}
+CFG = {
+    "KG": ["avavaaav"] + ["aaaaaaav"] * 5,
+    "XR": ["ffffaaad"] * 6,
+    "XA": ["av"] * 6,
+    "SP0": "ppppvvvv",
+}
 
 SB = {
-    "kint": ([128, B], I32), "K0": ([128, B], F32), "K": ([128, W + L], F32), "KB": ([128, W], F32),
+    "kint": ([128, B], I32), "K0": ([128, B], F32), "K": ([128, PAD + W], F32), "KB": ([128, W], F32),
     "X": ([128, W], BF), "XQ1": ([128, W - L], BF), "XQ2": ([128, W - L], BF), "XQ3": ([128, W - L], BF),
-    "kvb0": ([128, 2048], F32), "kvb1": ([128, 2048], F32), "xvb0": ([128, 2048], BF), "xvb1": ([128, 2048], BF),
-    "pI": ([128, 8], I32), "pF": ([128, 16], F32), "J": ([128, 256], F32), "JB": ([128, 256], F32),
-    "J16": ([128, 256], F16), "RM": ([128, 16], F32), "Blk": ([128, 16], F32), "Blk16": ([128, 8], F16), "IW": ([128, 176], F32),
-    "Ib": ([128, 128], BF), "nIb": ([128, 128], BF), "hIb": ([128, 128], BF), "oneb": ([128, 128], BF),
-    "Dm": ([128, 256], BF), "wt": ([128, 256], F32), "Mm": ([128, 256], BF), "repl": ([128, 16], U16),
-    "RR": ([128, 64], BF), "RE": ([128, 192], BF), "CE": ([128, 64], F32), "tmpc": ([128, 512], F32),
-    "MA": ([128, 176], F16), "MB": ([128, 256], F32), "MC": ([128, 176], F32),
-    "W32": ([128, 16 if ACT16 else 16 * 144], F32), "W16": ([128, 16 * 144], F16), "QW": ([128, 4 * 176], BF),
-    "kc": ([128, 512], F16), "one16": ([128, 128], F16), "kca": ([128, 128], F16), "qc": ([128, 256], BF),
-    "CM": ([128, 6 * 128], F16), "CA": ([128, 6 * 128], F16), "BI": ([128, 32], F32),
+    "kvb0": ([128, 1024], F32), "kvb1": ([128, 1024], F32), "xvb0": ([128, 1024], BF), "xvb1": ([128, 1024], BF),
+    "G16": ([128, 4096], F16), "Xc": ([128, 6144], BF), "Dab": ([128, 4096], BF), "eq": ([128, 6144], BF),
+    "Mx": ([128, R * 2048], BF), "l1": ([128, 512], U16), "l2": ([128, 256], U16), "hi": ([128, 384], BF), "lo": ([128, 384], BF),
+    "mW": ([128, 16], F32),
+    "pI": ([128, 8], I32), "pF": ([128, 32], F32), "J": ([128, 256], F32), "JB": ([128, 256], F32),
+    "J16": ([128, 256], F16), "RM": ([128, 16], F32), "Blk": ([128, 8], F32), "Blk16": ([128, 8], F16), "Blkb": ([128, 8], BF),
+    "IW": ([128, 176], F16), "I32": ([128, 128], F32), "MP": ([128, 4 * 176], F16), "W16": ([128, 16 * 144], F16),
+    "SEL": ([128, 128], F16), "Ib": ([128, 128], BF), "nIb": ([128, 128], BF), "hIb": ([128, 128], BF), "o4k": ([128, 128], BF),
+    "Dm": ([128, 256], BF), "wt": ([128, 256], F32), "Mm": ([128, 256], BF), "repl": ([128, 16], U16), "rep4": ([128, 16], U16),
+    "RR": ([128, 80], BF), "RX": ([128, 128], BF), "RE": ([128, 192], BF), "CE": ([128, 64], F32), "tmpc": ([128, 256], F32),
+    "I16": ([128, 128], BF), "kc": ([128, 512], BF), "oneb": ([128, 128], BF), "kca": ([128, 128], BF),
+    "qc": ([128, 272], BF), "CM": ([128, 3 * 128], F16), "CM32": ([128, 128], F32), "CA": ([128, 6 * 128], F16),
+    "BI": ([128, 32], F32), "VN": ([128, 256], F32),
     "wI": ([128, 8], I32), "wF": ([128, 8], F32), "wS": ([128, 48], BF), "thI": ([128, 48], I32), "thF": ([128, 48], F32),
-    "thB": ([128, 48], F32), "thz": ([128, 16], F32), "zF": ([128, 8], F32), "zI": ([128, 8], I32),
+    "thB": ([128, 48], F32), "thz": ([128, 16], F32), "zF": ([128, 32], F32),
     "aI": ([128, 96], I32), "aJ": ([128, 96], I32), "aL": ([128, 256], F16), "aU": ([128, 96], U16),
     "aR": ([128, 96], U16), "dS": ([128, R * L], F32), "dR": ([128, R * L], F32),
-    "scn": ([128, 512], F32), "rst": ([128, 512], F32),
-    "kI": ([128, 32], I32), "kJ": ([128, 32], I32), "sm": ([128, 160], F32), "mT": ([128, 16], F32), "nk": ([128, 16], BF),
-    "lost": ([128, 16], F32), "LM": ([128, 256], F16), "LR": ([128, 256], HF), "IH": ([128, 128], HF), "mW": ([128, 16], F32),
+    "scn": ([128, 768], F32), "rst": ([128, 256], F32), "rsa": ([128, 128], F32), "sd": ([128, 64], F32),
+    "F": ([128, 64], F32), "mT": ([128, 64], F32), "nk": ([128, 16], BF), "MZ": ([128, 32], F32), "zz": ([128, 32], F32),
+    "lost": ([128, 16], BF), "LM": ([128, 256], F16), "LR": ([128, 256], F16),
     "mR": ([128, 256], F16), "E": ([128, 16 * 256], BF), "Lw": ([128, 256], BF), "Lr": ([128, 256], BF),
-    "uL": ([128, 96], U16), "kv16": ([128, 256], F16), "km16": ([128, 256], F16), "xm": ([128, 256], BF),
-    "KW": ([128, 768], F32), "SW": ([128, 768], F32), "XW": ([128, 832], BF), "kmN": ([128, 256], F32),
+    "uL": ([128, 80], U16), "kv16": ([128, 256], F16), "ks16": ([128, 256], F16), "km": ([128, 256], F32), "xm": ([128, 256], BF),
+    "KW": ([128, 768], F32), "SW": ([128, 768], F32), "XW": ([128, 512], BF),
     "pk": ([128, 256], F32), "pc": ([128, 512], F32), "pr": ([128, 64], F32), "xc": ([128, 64], BF), "dU": ([128, 64], U16),
     "Xa": ([128, 1024], BF), "Da": ([128, 1024], BF), "asn": ([128, 128], F32), "bI": ([128, 8], I32), "bJ": ([128, 8], I32),
     "bL": ([128, 128], F16), "nBR": ([128, 128], F16),
 }
-for _s in "SD":
-    if not ACT16:
-        SB["G32" + _s] = ([128, 2048], F32)
-    if ACT16 or ADVE[_s]:
-        SB["G16" + _s] = ([128, 2048 if ACT16 else 1024 * ADVE[_s]], F16)
-    for _n, _d in (("Xc", BF), ("Dab", BF), ("Dsg", BF), ("eq", BF)):
-        if _n != "Dsg" or "d" in ROUTE[_s]:
-            SB[_n + _s] = ([128, 2048], _d)
-    SB["l1" + _s] = ([128, 128], U16)
-    SB["l2" + _s] = ([128, 128], U16)
-    SB["hi" + _s] = ([128, 128], BF)
-    SB["lo" + _s] = ([128, 128], BF)
-PS = ["key0", "key1", "pS", "pD1", "pD2", "pT1", "pT2", "pT3"]
+PS = ["bS", "bD", "pX1", "pX2", "pT1", "pT2", "pT3", "bF"]
 SCRATCH = {k: ("sbuf", v[0], v[1]) for k, v in SB.items()}
 for _p in PS:
     SCRATCH[_p] = ("psum", [128, 512], F32)
 
 ENG = ["pe", "dve", "act", "pool", "sp"]
 XSEND = [(u, d) for u in range(R - 1) for d in (1, 2, 3) if any(t % 3 + 1 == d for t in range(u + 1, R))]
-SEMAPHORES = (["c_" + e for e in ENG[:4]] + ["d%d" % i for i in range(60)] + ["sent"] + ["xi%d" % d for d in (1, 2, 3)]
-              + ["al%d" % d for d in (1, 2, 3)] + ["dq%d" % t for t in range(R)] + ["xn%d_%d" % ud for ud in XSEND])
+SEMAPHORES = (["c_" + e for e in ENG[:4]] + ["d%d" % i for i in range(48)] + ["sent"] + ["xi%d" % d for d in (1, 2, 3)]
+              + ["al%d" % d for d in (1, 2, 3)] + ["dq%d" % t for t in range(R)] + ["xn%d_%d" % ud for ud in XSEND]
+              + ["%s%d_%d" % (s, t, p) for s in ("fo", "fb") for t in range(R) for p in range(2)])
 
-CYC, GA, SC, PEC = 1.04, 1.56, 3.8, 0.52
-HOP = 150.0
+NOMINAL = (1.15, 1.56, 3.8, 0.42, 150.0, 500.0)
+OTHERS = [(1.0, 1.56, 3.8, 0.42, 150.0, 400.0), (1.1, 1.15, 2.5, 0.42, 150.0, 600.0), (1.4, 1.9, 5.0, 0.42, 150.0, 600.0),
+          (1.25, 1.3, 5.0, 0.42, 200.0, 800.0)]
+
+
+def price(o, m):
+    fix, cyc, ga, sc, pe, raw = o["c"]
+    return m[0] * (fix + 0.83 * (cyc + ga * m[1] + sc * m[2]) + pe * m[3]) + raw + (m[5] if "rem" in o else 0.0)
+
+
+def helper_of(T, topo, core):
+    same = [c for c in topo.cores_of(core) if topo.die(c) == topo.die(core)]
+    return [c for c in same if c not in T.cores][[c for c in same if c in T.cores].index(core)]
+
+
+def mask_of(topo, src, dst, ne):
+    mask = 0
+    for e in topo.engines(src, dst)[:ne]:
+        mask |= 1 << e
+    return mask
 
 
 def build(T, topo, core, rank):
@@ -78,9 +93,6 @@ def build(T, topo, core, rank):
         w = 4 if name in PS else SZ[SB[name][1]]
         return {"ap": T[name][ps, cs], "reg": [(name, a, b, st or 1)], "n": n, "w": w, "ps": name in PS}
 
-    def V4(name, idx, n):
-        return {"ap": T[name][idx], "reg": [(name, 0, 1 << 20)], "n": n, "w": SZ[SB[name][1]], "ps": False}
-
     def IND(win, off):
         return {"ap": win["ap"].indirect(off["ap"]), "reg": win["reg"] + off["reg"], "n": 16 * off["n"], "w": 4,
                 "ps": False, "ind": True, "off": off["reg"], "win": win["reg"]}
@@ -95,23 +107,23 @@ def build(T, topo, core, rank):
                 r += x["reg"]
         return r
 
-    def add(eng, fn, rd, wr, cost, **kw):
-        o = {"eng": eng, "fn": fn, "rd": rd, "wr": wr, "cost": cost, "id": len(ops)}
+    def add(eng, fn, rd, wr, c, **kw):
+        o = {"eng": eng, "fn": fn, "rd": rd, "wr": wr, "c": c, "id": len(ops)}
         o.update(kw)
         ops.append(o)
         return o
 
     def vcost(out, ins, two):
         if out.get("ind"):
-            return 50 + out["n"] * SC * CYC
+            return (40, 0, 0, out["n"], 0, 0)
         if ins[0].get("ind"):
-            return 50 + out["n"] * GA * CYC
+            return (40, 0, out["n"], 0, 0, 0)
         f = 1.0
         if two and not any(x["ps"] for x in ins):
             f = 2.0
         elif not two and out["w"] == 2 and all(x["w"] == 2 for x in ins):
             f = 0.5
-        return 20 + max(64, out["n"] * f) * CYC
+        return (16, max(64, out["n"] * f), 0, 0, 0, 0)
 
     def vadd(fn, out, ins, extra, two):
         rd = regs(ins + extra)
@@ -124,12 +136,8 @@ def build(T, topo, core, rank):
     def cp(out, a):
         vadd(lambda g: g.vector.tensor_copy(out["ap"], a["ap"]), out, [a], [], False)
 
-    setup = [False]
-
     def ts(out, a, s1, o1, s2=None, o2=None):
-        if setup[0] and o2 is None and o1 == ALU.mult and a["n"] >= setup[0]:
-            act(out, a, AF.Copy, None, s1)
-        elif o2 is None:
+        if o2 is None:
             vadd(lambda g: g.vector.tensor_scalar(out["ap"], a["ap"], ap(s1), None, o1), out, [a], [s1], False)
         else:
             vadd(lambda g: g.vector.tensor_scalar(out["ap"], a["ap"], ap(s1), ap(s2), o1, o2), out, [a], [s1, s2], False)
@@ -142,6 +150,7 @@ def build(T, topo, core, rank):
 
     def ms(out, c):
         vadd(lambda g: g.vector.memset(out["ap"], c), out, [out], [], False)
+        ops[-1]["rd"] = []
 
     def act(out, a, func=AF.Copy, bias=None, scale=None):
         kw = {}
@@ -149,8 +158,17 @@ def build(T, topo, core, rank):
             kw["bias"] = ap(bias)
         if scale is not None:
             kw["scale"] = ap(scale)
-        c = 65 + out["n"] * (GA if a.get("ind") else 1.0) * CYC
+        c = (52, 0, out["n"], 0, 0, 0) if a.get("ind") else (52, out["n"], 0, 0, 0, 0)
         add("act", lambda g: g.scalar.activation(out["ap"], a["ap"], func, **kw), regs([a, bias, scale]), out["reg"], c)
+
+    def scale(out, a, s):
+        act(out, a, AF.Copy, None, s)
+
+    def shifted(q, out, a, c):
+        if q == "a":
+            act(out, a, AF.Copy, c)
+        else:
+            ts(out, a, c, ALU.add)
 
     def mm(items):
         def fn(g):
@@ -158,24 +176,27 @@ def build(T, topo, core, rank):
             for o, l, r, s0, s1 in items:
                 ins = g.tensor.matmul(o["ap"], l["ap"], r["ap"], s0, s1)
             return ins
-        c = 30.0
+        c = 0
         rd, wr = [], []
         for o, l, r, s0, s1 in items:
-            c += max(min(64, l["n"]), r["n"]) * (4 if r["w"] == 4 else 1) * PEC
+            c += max(min(64, l["n"]), r["n"]) * (4 if r["w"] == 4 else 1)
             rd += l["reg"] + r["reg"]
             wr += o["reg"]
-        add("pe", fn, rd, wr, c)
+        add("pe", fn, rd, wr, (24, 0, 0, 0, c, 0))
 
     def grp(out, pairs, first=True, last=True):
         mm([(out, l, r, first and i == 0, last and i == len(pairs) - 1) for i, (l, r) in enumerate(pairs)])
 
     def iota(out, pat, base=0, cm=0, fl=True):
         kw = {"allow_small_or_imprecise_dtypes": True} if fl else {}
-        add("pool", lambda g: g.iota(out["ap"], pat, base, cm, **kw), [], out["reg"], 130 + 2 * CYC * out["n"])
+        add("pool", lambda g: g.iota(out["ap"], pat, base, cm, **kw), [], out["reg"], (130, 2 * out["n"], 0, 0, 0, 0))
+
+    def psel(out, a, pat, base):
+        add("pool", lambda g: g.affine_select(out["ap"], a["ap"], pat, ALU.is_ge, 0.0, base, 0),
+            a["reg"], out["reg"], (170, 2 * out["n"], 0, 0, 0, 0))
 
     def pcopy(out, a):
-        add("pool", lambda g: g.affine_select(out["ap"], a["ap"], [[0, out["n"]]], ALU.is_ge, 0.0, 1, 0),
-            a["reg"], out["reg"], 170 + 2 * CYC * out["n"])
+        psel(out, a, [[0, out["n"]]], 1)
 
     nd = [0]
 
@@ -188,25 +209,40 @@ def build(T, topo, core, rank):
             for o, i in pairs:
                 e.dma_start(o, i).then_inc(T.sem[sem], 16)
             return None
-        add(q, fn, rd, wr, 60.0 * len(pairs), lat=1800 + nbytes / 150.0, sem=sem, cnt=16 * len(pairs))
+        add(q, fn, rd, wr, (0, 0, 0, 0, 0, 60.0 * len(pairs)), lat=1800 + nbytes / 150.0, sem=sem, cnt=16 * len(pairs))
 
     def send(dst_rank, out, a, sem, ne=16):
         dst = T.cores[dst_rank % N]
         rid, pid = topo.addr(dst)[:2]
-        mask = 0
-        for e in topo.engines(core, dst)[:ne]:
-            mask |= 1 << e
+        mask = mask_of(topo, core, dst, ne)
         o = add("pool", lambda g: g.remote_dma(out["ap"], a["ap"], T.sem[sem], T.sem.sent, pid, rid, mask),
-                a["reg"], [], 400.0, rem=ne)
-        add("recv", None, [], out["reg"], 0.0, lat=2500 + 128 * a["n"] * a["w"] / 120.0, sem=sem, cnt=ne, after=o["id"])
+                a["reg"], [], (0, 0, 0, 0, 0, 0), rem=ne)
+        add("recv", None, [], out["reg"], (0, 0, 0, 0, 0, 0), lat=2500 + 128 * a["n"] * a["w"] / 120.0, sem=sem, cnt=ne,
+            after=o["id"])
+
+    def fold(out, a, b, tag):
+        dst = helper_of(T, topo, core)
+        rid, pid = topo.addr(dst)[:2]
+        mask = mask_of(topo, core, dst, 16)
+
+        def fn(g):
+            tr = RemoteDMATransfer(dst_ids=[DstId(rid=rid, pnc=pid)], dma_engine_mask=mask, remote_sem=T.sem["fo" + tag],
+                                   srcs=[a["ap"], b["ap"]], dsts=[out["ap"]], alu_op=2)
+            return g.remote_dma_fused([tr], local_sem=T.sem["fb" + tag])
+        o = add("pool", fn, a["reg"] + b["reg"], [("folds", 0, 1)], (0, 0, 0, 0, 0, 0), rem=0)
+        add("recv", None, a["reg"] + b["reg"], out["reg"], (0, 0, 0, 0, 0, 0), lat=5000 + 3 * 128 * a["n"] * a["w"] / 200.0,
+            sem="fb" + tag, cnt=32, after=o["id"])
 
     yk, yx = T.yk, T.yx
     col = lambda name, j: V(name, j, j + 1)
+    one = (0, 1)
+    Kp = lambda c0, c1, st=None: V("K", PAD + c0, PAD + c1, st)
 
-    hb = B // 2
-    dma([(T.kint[:, 0:hb], T.kin[:, 0:hb])], [], [("kint", 0, hb)], 128 * hb * 4)
-    dma([(T.kint[:, hb:B], T.kin[:, hb:B])], [], [("kint", hb, B)], 128 * hb * 4, q="act")
-    dma([(T.X[:, 0:B], T.xf[:])], [], [("X", 0, B)], 128 * B * 2)
+    qb = B // 4
+    for q in range(4):
+        dma([(T.kint[:, qb * q:qb * q + qb], T.kin[:, qb * q:qb * q + qb])], [], [("kint", qb * q, qb * q + qb)],
+            128 * qb * 4 * (q + 1) * 0.6, q=("sp", "act")[q % 2])
+    dma([(T.X[:, 0:B], T.xf[:])], [], [("X", 0, B)], 128 * B * 2 * 1.6)
     dma([(T.wI[:, 0:6], T.w[:]), (T.thI[0:1, 0:48], T.th[:])], [], [("wI", 0, 8), ("thI", 0, 48)], 4096)
 
     iota(col("pI", 0), [[0, 1]], 0, 1, False)
@@ -219,135 +255,132 @@ def build(T, topo, core, rank):
     ts(col("pF", 3), col("pF", 0), 16.0, ALU.add)
     ts(V("IW"), V("J", 0, 176), col("pF", 3), ALU.is_equal)
     ts(V("RM"), V("J", 0, 16), pr, ALU.is_equal)
-    I32v = V("IW", 16, 144)
-    ts(col("pF", 4), pr, 9.0, ALU.is_ge)
-    ts(col("pF", 5), pr, 8.0, ALU.is_ge)
-    ts(col("pF", 6), pr, 8.0, ALU.is_lt)
-    tt(col("pF", 7), col("pF", 4), col("RM", 0), ALU.add)
-    ts(col("pF", 7), col("pF", 7), -1.0, ALU.mult, 1.0, ALU.add)
-    tt(col("pF", 8), col("RM", 6), col("RM", 7), ALU.add)
-    ts(col("pF", 9), col("pF", 8), -1.0, ALU.mult, 1.0, ALU.add)
-    ts(col("pF", 10), pr, 6.0, ALU.is_le, BIG, ALU.mult)
-    setup[0] = 8 if ACT16 else False
-    ts(V("tmpc", 0, 176), V("IW"), col("pF", 4), ALU.mult)
-    ts(V("MC"), V("IW"), col("RM", 0), ALU.mult)
-    for h in range(2):
-        tt(V("MB", 128 * h, 128 * h + 128), V("tmpc", 25 - 8 * h, 153 - 8 * h), V("MC", 9 - 8 * h, 137 - 8 * h), ALU.add)
-    ts(V("MA"), V("IW"), col("pF", 7), ALU.mult)
+    IH = V("IW", 16, 144)
+    ts(V("pF", 4, 8), V("J", 0, 16, 4), 1.0, ALU.add, pr, ALU.is_le)
+    tt(V("pF", 8, 11), V("pF", 4, 7), V("pF", 5, 8), ALU.subtract)
+    for p, c in enumerate((10, 7, 8, 9)):
+        ts(V("MP", 176 * p, 176 * p + 176), V("IW"), col("pF", c), ALU.mult)
     for r in range(16):
-        if not ACT16:
-            act(V("W32", 144 * r, 144 * r + 144), V("IW", r + 1, r + 145), AF.Copy, None, col("RM", r))
         ts(V("W16", 144 * r, 144 * r + 144), V("IW", r + 1, r + 145), col("RM", r), ALU.mult)
-    w32 = lambda r, b: V("W32", 144 * r + 15 - b, 144 * r + 143 - b)
     w16 = lambda r, b: V("W16", 144 * r + 15 - b, 144 * r + 143 - b)
     iota(V("KB", 0, B), [[0, B // 8], [1, 8]])
     ops[-1]["rd"] = [("JB", 0, 256), ("J", 0, 256)]
-    cp(V("K0", 0, hb), V("kint", 0, hb))
-    cp(V("K0", hb, B), V("kint", hb, B))
+    for q in range(4):
+        cp(V("K0", qb * q, qb * q + qb), V("kint", qb * q, qb * q + qb))
 
-    def kbcopy(src, c0, c1):
-        dma([(T.KB[16 * g:16 * g + 6, c0:c1], T[src][16 * g:16 * g + 6, c0:c1]) for g in range(8)],
-            [(src, c0, c1)], [("KB", c0, c1)], 48 * (c1 - c0) * 4)
-    kbcopy("K0", 0, B)
-    dma([(T.K[:, 0:B], T.K0[:])], [("K0", 0, B), ("KB", 0, B)], [("K", 0, B)], 128 * B * 4)
-    ts(V("Blk", 0, 8), V("J", 0, 8), pg, ALU.is_equal)
-    ts(V("Blk", 8, 16), V("J", 0, 8), pg, ALU.is_gt)
-    blk, slt = V("Blk", 0, 8), V("Blk", 8, 16)
-    cp(V("Blk16"), blk)
-    act(V("Ib"), I32v)
-    act(V("nIb"), I32v, AF.Copy, None, -1.0)
-    act(V("hIb"), I32v, AF.Copy, None, 0.5)
-    for h in range(2):
-        for wi in range(2):
-            q = 2 * h + wi
-            ts(V("QW", 176 * q, 176 * q + 176), V("IW"), col("pF", 6 - h), ALU.mult, (0.0625, 1.0)[wi], ALU.mult)
-    for wi in range(2):
-        ts(V("RR", 8 * wi, 8 * wi + 8), blk, 4096.0, ALU.mult)
-        ts(V("RR", 16 + 8 * wi, 24 + 8 * wi), blk, col("pF", 10), ALU.mult)
-        ts(V("RR", 32 + 8 * wi, 40 + 8 * wi), blk, -4096.0, ALU.mult)
-    ts(V("RR", 48, 56), blk, 16.0, ALU.mult)
-    cp(V("repl"), V("J", 0, 16))
-    one = (0, 1)
-    for h in range(2):
-        iota(V("tmpc", 256 * h, 256 * h + 256, p=one), [[-120, 2], [0, 8], [256, 16]], 256 * 9 + 128)
-    ts(V("scn", 0, 256, p=one), V("JB", p=one), 7.0, ALU.is_ge, -4096.0, ALU.mult)
-    for h in range(2):
-        tt(V("kc", 256 * h, 256 * h + 256, p=one), V("tmpc", 256 * h, 256 * h + 256, p=one), V("scn", 0, 256, p=one), ALU.add)
-    ms(V("one16", p=one), 1.0)
-    for s in "SD":
-        if "d" in ROUTE[s]:
-            for c in range(4):
-                if ROUTE[s][c] != "d":
-                    ms(V("Dsg" + s, 512 * c, 512 * c + 512), 0.0)
+    def kbcopy(src, o, c0, c1):
+        dma([(T.KB[r:128:16, c0:c1], T[src][r:128:16, o + c0:o + c1]) for r in range(6)],
+            [(src, o + c0, o + c1)], [("KB", c0, c1)], 48 * (c1 - c0) * 4)
+    kbcopy("K0", 0, 0, B)
+    dma([(T.K[:, PAD:PAD + B], T.K0[:]), (T.K[:, 0:PAD], T.K0[:, 0:PAD])], [("K0", 0, B), ("KB", 0, B)], [("K", 0, PAD + B)],
+        128 * B * 4)
+    ts(col("pF", 11), pr, 8.0, ALU.mult, pg, ALU.add)
+    ts(V("SEL"), V("J", 0, 128), col("pF", 11), ALU.is_equal, 0.0625, ALU.mult)
+    ts(V("Blk"), V("J", 0, 8), pg, ALU.is_equal)
+    blk = V("Blk")
+    act(V("Ib"), IH)
+    scale(V("nIb"), IH, -1.0)
+    scale(V("RR", 0, 16, 2), blk, 4096.0)
+    scale(V("RR", 1, 16, 2), blk, 4096.0)
+    scale(V("I16"), IH, 16.0)
+    ts(col("pF", 12), pr, 6.0, ALU.is_le, BIG, ALU.mult)
+    ts(V("RR", 16, 32), V("RR", 0, 16), 0.0, ALU.is_gt, col("pF", 12), ALU.mult)
+    scale(V("RR", 32, 48), V("RR", 0, 16), -1.0)
+    scale(V("RR", 48, 64), V("RR", 0, 16), 2.0)
+    rs, rb, rn, r2 = (V("RR", 16 * j, 16 * j + 16) for j in range(4))
+    ms(V("oneb", p=one), 1.0)
+    ones = V("oneb", p=one)
+    iota(V("kc", p=one), [[-2048, 2], [0, 32], [256, 8]], 2304)
+    psel(V("kc", 0, 256, p=one), V("kc", 0, 256, p=one), [[0, 32], [-1, 8]], 6)
+    iota(V("tmpc", 0, 128), [[1, 8], [0, 16]])
+    ts(V("nBR"), V("tmpc", 0, 128), pg, ALU.is_equal, -1.0, ALU.mult)
+    scale(V("RX"), V("nBR"), 4096.0)
+    ms(V("rst"), -1e9)
+    ms(V("rst", 0, 256, 8), 16777216.0)
     for d in (1, 2, 3):
         send(rank - d, V("XQ%d" % d, 0, B), V("X", 0, B), "xi%d" % d)
-        ops[-2]["rd"] = ops[-2]["rd"] + [("KB", 0, B)]
+        ops[-2]["rd"] = ops[-2]["rd"] + [("KB", 0, B)] + ([("scn", 0, 256)] if d > 1 else [])
     iota(V("KB", B, W), [[0, (W - B) // 8], [1, 8]])
 
     def late_constants():
-        act(V("IH"), I32v)
-        cp(V("RR", 56, 64), blk)
-        ms(V("oneb"), 1.0)
+        scale(V("hIb"), IH, 0.5)
+        act(V("I32"), IH)
+        cp(V("Blk16"), blk)
+        act(V("Blkb"), blk)
+        scale(V("RR", 64, 72), blk, 16.0)
+        cp(V("repl"), V("J", 0, 16))
+        ts(V("rep4"), V("J", 0, 16), 4.0, ALU.mult, 3.0, ALU.add)
+        ms(V("o4k"), 4096.0)
         ts(V("Dm"), V("JB"), pr, ALU.is_equal)
         ts(V("wt"), V("JB"), pr, ALU.is_gt)
-        act(V("tmpc", 0, 256), V("Dm"), AF.Copy, None, EW)
-        tt(V("wt"), V("wt"), V("tmpc", 0, 256), ALU.add)
+        scale(V("pk"), V("Dm"), EW)
+        tt(V("wt"), V("wt"), V("pk"), ALU.add)
         ts(V("Mm"), V("JB"), pr, ALU.is_le, 8192.0, ALU.mult)
-        for h in range(2):
-            ts(V("rst", 256 * h, 256 * h + 256), V("JB"), 0.0, ALU.is_equal, 1e9, ALU.mult)
-        ms(V("RE"), 0.0)
-        for ri, wv in enumerate((1.0 / 4096, 1.0, -1.0)):
-            for h in range(2):
-                c = 16 * ri + 8 * h
-                ts(V("RE", 48 * h + c, 48 * h + c + 8), blk, wv, ALU.mult)
-                ts(V("RE", 96 + 48 * h + c, 96 + 48 * h + c + 8), slt, wv, ALU.mult)
-            ms(V("RE", 96 + 16 * ri + 8, 96 + 16 * ri + 16), wv)
+        ms(V("rsa"), 0.0)
+        ms(V("rsa", 0, 128, 16), 1e9)
+        ms(V("sd"), -1.0)
+        ms(V("sd", 0, 64, 4), 0.0)
+        ms(V("sd", 2, 64, 4), -16.0)
+        ts(col("pF", 13), pg, 8.0, ALU.add)
+        for j, (cmp, c) in enumerate(((ALU.is_equal, pg), (ALU.is_equal, col("pF", 13)), (ALU.is_gt, pg), (ALU.is_gt, col("pF", 13)))):
+            ts(V("RE", 48 * j, 48 * j + 16), V("JB", 0, 16), c, cmp, 1.0 / 4096, ALU.mult)
+            ts(V("RE", 48 * j + 16, 48 * j + 48), V("JB", 0, 32), c, cmp, -1.0, ALU.mult)
         ts(V("CE", 48, 64), V("J", 0, 16), 16.0, ALU.mult, pr, ALU.add)
-        ts(V("CE", 0, 16), V("CE", 48, 64), 3.0, ALU.mult, -(0.5 - 1.0 / 8192), ALU.add)
-        ms(V("CE", 16, 32), 0.0)
-        ts(V("CE", 32, 48), V("CE", 48, 64), 256.0, ALU.add)
-        ts(V("CE", 48, 64), V("CE", 48, 64), 16.0, ALU.mult)
-        cp(V("J16"), V("J"))
-        cp(V("kca", p=one), V("JB", 0, 128, p=one))
+        act(V("CE", 0, 16), V("CE", 48, 64), AF.Copy, -(0.5 - 1.0 / 8192), 3.0)
+        act(V("CE", 16, 48), V("J", 0, 32), AF.Copy, EW + 255.0, 0.0)
+        act(V("MZ", 16, 32), V("CE", 48, 64), AF.Copy, 256.0)
+        scale(V("CE", 48, 64), V("CE", 48, 64), 16.0)
+        act(V("J16"), V("J"))
+        act(V("kca", p=one), V("JB", 0, 128, p=one))
         ms(V("qc", p=one), -0.25)
+        ms(V("qc", 256, 272, p=one), 1920.0 / 4096)
         cm = lambda j: V("CM", 128 * j, 128 * j + 128)
-        tt(cm(0), w16(0, 2), w16(1, 3), ALU.add)
-        tt(cm(0), cm(0), w16(7, 8), ALU.add)
-        ts(cm(1), I32v, col("pF", 4), ALU.mult)
-        tt(cm(1), cm(1), w16(0, 4), ALU.add)
-        tt(cm(1), cm(1), w16(1, 5), ALU.add)
-        ts(col("pF", 11), col("RM", 0), 8.0, ALU.mult, col("pF", 8), ALU.add)
-        ts(cm(2), I32v, col("pF", 11), ALU.mult)
-        ts(cm(3), I32v, col("pF", 9), ALU.mult)
-        ts(col("pF", 12), col("RM", 6), 8.0, ALU.mult, col("RM", 7), ALU.add)
-        ts(cm(4), I32v, col("pF", 12), ALU.mult)
+        r67, n67 = col("pF", 14), col("pF", 15)
+        tt(r67, col("RM", 6), col("RM", 7), ALU.add)
+        ts(n67, r67, -1.0, ALU.mult, 1.0, ALU.add)
+        grp(V("pT2", 0, 128), [(IH, w16(0, 2)), (IH, w16(1, 3)), (IH, w16(7, 8))])
+        act(cm(0), V("pT2", 0, 128))
+        grp(V("pT2", 128, 256), [(IH, w16(0, 4)), (IH, w16(1, 5)), (IH, V("MP", 16, 144)), (IH, V("MP", 192, 320))])
+        act(V("CM32"), V("pT2", 128, 256))
+        ts(col("pF", 16), col("RM", 0), 8.0, ALU.mult, r67, ALU.add)
+        ts(cm(1), IH, col("pF", 16), ALU.mult)
+        ts(cm(2), IH, n67, ALU.mult)
+        ts(col("pF", 17), col("RM", 6), 8.0, ALU.mult, col("RM", 7), ALU.add)
+        scale(V("VN"), V("J"), col("pF", 17))
+        ts(V("pF", 24, 30), V("RM", 9, 15), -1.0, ALU.mult, 1.0, ALU.add)
         for t in range(R):
-            tt(V("CA", 128 * t, 128 * t + 128), I32v, w16(9 + t, 9 + t), ALU.subtract)
+            ts(V("CA", 128 * t, 128 * t + 128), IH, col("pF", 24 + t), ALU.mult)
         j6 = V("J", 0, 6)
-        for kind, (mv, mn) in enumerate(((col("RM", 0), col("pF", 8)), (None, col("RM", 7)), (col("RM", 6), col("RM", 7)))):
-            ts(col("pF", 13), mn, 256.0, ALU.mult)
-            ts(col("pF", 14), col("pF", 13), 2048.0, ALU.add)
-            if mv is not None:
-                tt(col("pF", 13), col("pF", 13), mv, ALU.add)
-                ts(col("pF", 14), mv, -2048.0, ALU.mult, col("pF", 14), ALU.add)
-            ts(V("BI", 8 * kind, 8 * kind + 6), j6, col("pF", 13), ALU.mult, col("pF", 14), ALU.add)
+        c18, c19, c20 = col("pF", 18), col("pF", 19), col("pF", 20)
+        ts(c18, col("RM", 0), col("RM", 1), ALU.add)
+        ts(c18, r67, 256.0, ALU.mult, c18, ALU.add)
+        ts(c19, col("RM", 2), col("RM", 3), ALU.add, col("RM", 8), ALU.add)
+        ts(c19, c19, 2048.0, ALU.mult)
+        ts(c19, r67, float(B), ALU.mult, c19, ALU.add)
+        ts(c19, col("RM", 1), float(MID), ALU.mult, c19, ALU.add)
+        ts(V("BI", 0, 6), j6, c18, ALU.mult, c19, ALU.add)
+        ts(c18, col("RM", 7), 256.0, ALU.mult, col("RM", 6), ALU.add)
+        ts(c20, col("RM", 7), float(B), ALU.mult)
+        ts(V("BI", 16, 22), j6, c18, ALU.mult, c20, ALU.add)
+        ts(c19, col("RM", 6), float(MID), ALU.mult)
+        ts(c19, n67, 2048.0, ALU.mult, c19, ALU.add)
+        ts(V("BI", 8, 14), V("BI", 16, 22), c19, ALU.add)
         ts(V("BI", 24, 30), j6, 256.0, ALU.mult, 256.0, ALU.add)
         tt(V("BI", 24, 30), V("BI", 24, 30), V("RM", 9, 15), ALU.mult)
         ts(V("BI", 24, 30), V("BI", 24, 30), 2048.0, ALU.add)
-        for q in range(4):
-            ms(V("E", 1024 * q, 1024 * q + 1024), 0.0)
-        ms(V("pc"), 0.0)
-        iota(V("tmpc", 256, 384), [[1, 8], [0, 16]])
-        ts(V("nBR"), V("tmpc", 256, 384), pg, ALU.is_equal, -1.0, ALU.mult)
+        ms(V("E", 0, 512), 0.0)
+        dma([(T.E[:, 512 * q:512 * q + 512], T.E[:, 0:512]) for q in range(1, 8)], [("E", 0, 512)], [("E", 512, 4096)], 128 * 7168)
+        iota(V("pc"), [[0, 512]])
         ms(V("bJ"), 0)
-        setup[0] = False
-        ts(V("thF", p=one), V("thI", p=one), 4096.0, ALU.mult)
-        add("pool", lambda g: g.partition_broadcast(T.thB[:], T.thF[0:1, :], 128), [("thF", 0, 48)], [("thB", 0, 48)], 400.0)
+        ts(V("thF", p=one), V("thI", p=one), 4081.0, ALU.min, 4096.0, ALU.mult)
+        add("pool", lambda g: g.partition_broadcast(T.thB[:], T.thF[0:1, :], 128), [("thF", 0, 48)], [("thB", 0, 48)],
+            (140, 192, 0, 0, 0, 0))
         for h in range(2):
-            cp(V("thz", 8 * h, 8 * h + 8), V("thB", 0, 48, 6))
+            act(V("thz", 8 * h, 8 * h + 8), V("thB", 0, 48, 6), AF.Copy, -128.0)
+        act(V("thB"), V("thB"), AF.Copy, 30720.0 - 128.0)
         cp(V("wF", 0, 6), V("wI", 0, 6))
         for t in range(R):
-            ts(V("wS", 8 * t, 8 * t + 8), blk, col("wF", t), ALU.mult)
+            scale(V("wS", 8 * t, 8 * t + 8), blk, col("wF", t))
         mm([(V("pT3", 16 * t + 8 * h, 16 * t + 8 * h + 8), xv(t, h), V("wS", 8 * t, 8 * t + 8), True, True)
             for t in range(R) for h in range(2)])
         cp(V("aI"), V("pT3", 0, 96))
@@ -364,98 +397,168 @@ def build(T, topo, core, rank):
         send(rank + d, V("aR", 32 * d - 32, 32 * d), V("aU", 32 * d - 32, 32 * d), "al%d" % d, 4)
 
     def lanes(name, t, h=None):
+        o = PAD if name == "K" else 0
         if h is None:
-            return V(name, t, 2048, 8)
-        return V(name, t + 1024 * h, 1024 * h + 1024, 8)
+            return V(name, o + t, o + 2048, 8)
+        return V(name, o + t + 1024 * h, o + 1024 * h + 1024, 8)
 
     def xv(t, h=None):
         return lanes("X", t, h)
 
-    def spread(name, src, t):
-        for b in range(16):
-            if t == 0 and (b % 3 == 0 or src == "X" and b % 3 == 1):
-                act(V(name, b, 2048, 16), lanes(src, t, b // 8))
-            elif t == 0 and (b % 3 == 1 or src == "X"):
-                cp(V(name, b, 2048, 16), lanes(src, t, b // 8))
-            else:
-                pcopy(V(name, b, 2048, 16), lanes(src, t, b // 8))
+    def spreads(t):
+        for j, (name, src) in enumerate((("xvb", "X"), ("kvb", "KB"))):
+            for kk in range(4):
+                q = CFG["SP0"][4 * j + kk] if t == 0 else "p"
+                {"p": pcopy, "a": act, "v": cp}[q](V(name + str(t % 2), kk, 1024, 4), lanes(src, t))
 
-    def batch(t, s):
-        a = slice(None)
-        cnt = B + L * t
-        still = s == "S" or t == 0
-        kt, wn = ("K0", B) if still else ("K", cnt)
-        key = "key%d" % (t % 2)
-        pe = "pS" if s == "S" else "pD1"
-        slot0 = 0 if s == "S" else 8
-        ks = [(slot0 + kk + 9) % 16 for kk in range(8)]
-        if s == "S":
-            mm([(V(key), V("one16", p=one), V("kc", p=one), True, False)])
-            grp(V(pe, 0, 128), [(V("MB", 128 * h, 128 * h + 128), lanes(kt, t, h)) for h in range(2)])
-            cp(V("l1" + s), V(pe, 0, 128))
-        else:
-            ts(V("kv16"), lanes(kt, t), -2048.0, ALU.add)
-            grp(V(pe, 0, 128), [(V("MA", 17 - 8 * h, 145 - 8 * h), V("kv16", 128 * h, 128 * h + 128)) for h in range(2)])
-            ts(V("l1" + s), V(pe, 0, 128), 2048.0, ALU.add)
-        for hf in range(2):
-            dv = hf < ADVE[s]
-            half = dv or ACT16
-            gb = ("G16" if half else "G32") + s
-            for c in (2 * hf, 2 * hf + 1):
-                src = IND(V(kt, 0, wn), V("l1" + s, 32 * c, 32 * c + 32))
-                if dv:
-                    ts(V(gb, 512 * c, 512 * c + 512), src, -2048.0, ALU.add)
-                else:
-                    act(V(gb, 512 * c, 512 * c + 512), src, AF.Copy, -2048.0)
-            st = 8 if half else 4
-            for b0 in range(0, 16, st):
-                grp(V(pe, 128 + 64 * hf, 192 + 64 * hf),
-                    [((w16 if half else w32)((ks[b % 8] + t) % 16, b), V(gb, 1024 * hf + b, 1024 * hf + 1024, 16))
-                     for b in range(b0, b0 + st)], b0 == 0, b0 + st == 16)
-        cP = V(pe, 128, 256)
-        ts(V("l2" + s), cP, 2048.0, ALU.add)
-        ts(V("hi" + s), cP, 16 * MAG0, ALU.add, 16 * MAG0, ALU.subtract)
-        tt(V("lo" + s), cP, V("hi" + s), ALU.subtract)
-        mm([(V(key, 256 * h + 128 * wi, 256 * h + 128 * wi + 128), V(("hi", "lo")[wi] + s),
-             V("QW", 176 * (2 * h + wi) + 16 - slot0 + 8 * h, 176 * (2 * h + wi) + 144 - slot0 + 8 * h), False, False)
-            for h in range(2) for wi in range(2)])
-        kvb, xvb = "kvb%d" % (t % 2), "xvb%d" % (t % 2)
-        for c in range(4):
-            off = V("l2" + s, 32 * c, 32 * c + 32)
-            cs = (512 * c, 512 * c + 512)
-            rt = ROUTE[s][c]
-            if rt == "a":
-                bank = "pS" if s == "S" else ("pD2", "pD1")[c % 2]
-                act(V("Xc" + s, *cs), IND(V("X", 0, wn), off))
-                grp(V(bank), [(V("Ib"), V("Xc" + s, *cs)), (V("nIb"), V(xvb, *cs))])
-                act(V("Dab" + s, *cs), V(bank), AF.Abs)
-            elif rt == "b":
-                tt(V("Xc" + s, *cs), IND(V("X", 0, wn), off), V(xvb, *cs), ALU.subtract)
-                act(V("Dab" + s, *cs), V("Xc" + s, *cs), AF.Abs)
-            else:
-                tt(V("Dsg" + s, *cs), IND(V("X", 0, wn), off), V(xvb, *cs), ALU.subtract)
-                ts(V("Dab" + s, *cs), V("Dsg" + s, *cs), 0.0, ALU.max, 2.0, ALU.mult)
-            tt(V("eq" + s, *cs), IND(V("KB", 0, wn), off), V(kvb, *cs), ALU.is_equal)
-        ko = lambda b: V(key, 256 * (b // 8) + slot0 + b % 8, 256 * (b // 8) + 256, 16)
-        for b0 in range(0, 16, 8):
-            mm([(ko(b), V("eq" + s, b, 2048, 16), V("RR", 16, 32), False, False) for b in range(b0, b0 + 8)])
-        if "d" in ROUTE[s]:
-            for b0 in range(0, 16, 8):
-                mm([(ko(b), V("Dsg" + s, b, 2048, 16), V("RR", 32, 48), False, False) for b in range(b0, b0 + 8)])
-        for b0 in range(0, 16, 8):
-            mm([(ko(b), V("Dab" + s, b, 2048, 16), V("RR", 0, 16), False, s == "D" and b == 15) for b in range(b0, b0 + 8)])
+    def first_list(t, p, src, out):
+        k0 = (9 + 4 * p) % 16
+        pairs = []
+        for lg in range(4):
+            o = 176 * p + 16 - (4 * lg - k0)
+            pairs.append((V("MP", o, o + 128), V(src, lg, 256, 4)))
+            if p == 1:
+                pairs.append((w16(0, 4 * lg + 3), V(src, lg, 256, 4)))
+        grp(out, pairs)
 
-    def tail(t):
+    def still_lists(t):
+        shifted("a", V("ks16"), lanes("K0", t), -2048.0)
+        for p in range(3):
+            first_list(t, p, "ks16", V("bF", 64 * p, 64 + 64 * p))
+        o = 256 * (t % 2)
+        ts(V("l1", o, o + 192), V("bF", 0, 192), 2048.0, ALU.add)
+
+    def relatives(t, p):
         cnt = B + L * t
+        still = p < 2 or t == 0 or (p == 2 and t == 1)
+        win = V("K0") if still else Kp(0, cnt)
+        bank = "bF" if p < 2 else "bD"
+        o = 256 * (t % 2) + 64 * p
+        if p == 3:
+            shifted("v", V("kv16"), lanes("K0" if t == 0 else "K", t), -2048.0)
+            first_list(t, p, "kv16", V(bank, 320, 384))
+            ts(V("l1", o, o + 64), V(bank, 320, 384), 2048.0, ALU.add)
+        for h in range(2):
+            shifted(CFG["KG"][t][2 * p + h], V("G16", 1024 * p + 512 * h, 1024 * p + 512 * h + 512),
+                    IND(win, V("l1", o + 32 * h, o + 32 * h + 32)), -float(MID + t))
+        row = [(9 + 4 * p + kk + t) % 16 for kk in range(4)]
+        lp = V(bank, 256 + 64 * (p % 2), 320 + 64 * (p % 2))
+        for b0 in (0, 8):
+            grp(lp, [(w16(row[b % 4], b), V("G16", 1024 * p + b, 1024 * p + 1024, 16)) for b in range(b0, b0 + 8)],
+                b0 == 0, b0 == 8)
+        ts(V("l2", 64 * p, 64 * p + 64), lp, float(MID + t), ALU.add)
+        mm([(V(bank, 384 + 64 * h + 4 * (p % 2) + kk, 448 + 64 * h, 8),
+             V("G16", 1024 * p + 512 * h + kk, 1024 * p + 512 * h + 512, 4), V("SEL", 8 * row[kk], 8 * row[kk] + 8), True, True)
+            for h in range(2) for kk in range(4)])
+
+    def split(t, s):
+        bank = ("bF", "bD")[s]
+        o = 256 if s else 128 * (t % 2)
+        ts(V("hi", o, o + 128), V(bank, 384, 512), MAG0, ALU.add, MAG0, ALU.subtract)
+        tt(V("lo", o, o + 128), V(bank, 384, 512), V("hi", o, o + 128), ALU.subtract)
+        mm([(V(("bS", "bD")[s], 0, 256), ones, V("kc", 256 * s, 256 * s + 256, p=one), True, False)])
+
+    def payload(t, s, last):
+        bank = ("bS", "bD")[s]
+        o = 256 if s else 128 * (t % 2)
+        for wi in range(2):
+            mm([(V(bank, 8 * wi + j, 256, 16), V(("Ib", "I16")[wi]), V(("hi", "lo")[wi], o + j, o + 128, 8), False,
+                 last and wi == 1 and j == 7) for j in range(8)])
+
+    def room(t, p):
+        return 1024 * (p + 2 * (t % 2) if p < 2 else p + 2)
+
+    def keyed(p, h, name, o, rhs, last=False):
+        bank = "bS" if p < 2 else "bD"
+        mm([(V(bank, 128 * h + 4 * (p % 2) + kk, 128 * h + 128, 8), V(name, o + 512 * h + kk, o + 512 * h + 512, 4), rhs,
+             False, last and kk == 3) for kk in range(4)])
+
+    def blood(t, p):
+        wn = B if p < 2 or t == 0 or (p == 2 and t == 1) else B + L * t
+        for h in range(2):
+            c = room(t, p) + 512 * h
+            tt(V("eq", c, c + 512), IND(V("KB", 0, wn), V("l2", 64 * p + 32 * h, 64 * p + 32 * h + 32)),
+               V("kvb%d" % (t % 2), 512 * h, 512 * h + 512), ALU.is_equal)
+
+    def feats(t, p):
+        wn = B if p < 2 or t == 0 or (p == 2 and t == 1) else B + L * t
+        xvb = "xvb%d" % (t % 2)
+        for h in range(2):
+            c = room(t, p) + 512 * h
+            dab = V("Dab", 1024 * p + 512 * h, 1024 * p + 512 * h + 512)
+            src = IND(V("X", 0, wn), V("l2", 64 * p + 32 * h, 64 * p + 32 * h + 32))
+            rt = CFG["XR"][t][2 * p + h]
+            if rt == "d":
+                tt(V("Xc", c, c + 512), src, V(xvb, 512 * h, 512 * h + 512), ALU.subtract)
+                ts(dab, V("Xc", c, c + 512), 0.0, ALU.max, 2.0, ALU.mult)
+                continue
+            bank = ("pX1", "pX2")[h]
+            if rt in "av":
+                mm([(V(bank), V("nIb"), V(xvb, 512 * h, 512 * h + 512), True, False)])
+            (act if rt in "af" else cp)(V("Xc", c, c + 512), src)
+            if rt in "av":
+                mm([(V(bank), V("Ib"), V("Xc", c, c + 512), False, True)])
+                act(dab, V(bank), AF.Abs)
+        if CFG["XR"][t][2 * p] in "fg":
+            o = 2048 * t + 1024 * p
+            fold(V("Mx", o, o + 1024), V("Xc", room(t, p), room(t, p) + 1024), V(xvb), "%d_%d" % (t, p))
+
+    def sums(t, p, last=False):
+        for h in range(2):
+            keyed(p, h, "eq", room(t, p), rb)
+        for h in range(2):
+            rt = CFG["XR"][t][2 * p + h]
+            if rt in "dfg":
+                keyed(p, h, "Xc", room(t, p), rn)
+            if rt in "fg":
+                keyed(p, h, "Mx", 2048 * t + 1024 * p, r2, last and h == 1)
+            else:
+                keyed(p, h, "Dab", 1024 * p, rs, last and h == 1)
+
+    def still(t):
+        still_lists(t)
+        for p in range(2):
+            relatives(t, p)
+            feats(t, p)
+            blood(t, p)
+        split(t, 0)
+        folded = [p for p in range(2) if CFG["XR"][t][2 * p] in "fg"]
+        if len(folded) == 2:
+            mm([(V("bS", 128 * h, 128 * h + 128), xv(t, h), V("RX"), False, False) for h in range(2)])
+        elif folded:
+            mm([(V("bS", 128 * h + 4 * folded[0] + kk, 128 * h + 128, 8), xv(t, h), rn, False, False)
+                for h in range(2) for kk in range(4)])
+        for p in sorted(range(2), key=lambda p: p in folded):
+            sums(t, p)
+        payload(t, 0, True)
+        scan(V("scn", 256 * (t % 2), 256 * (t % 2) + 256), V("rst"), V("bS", 0, 256), ALU.max, ALU.min)
+
+    def moving_a(t):
+        relatives(t, 2)
+        feats(t, 2)
+        blood(t, 2)
+
+    def moving_b(t):
+        relatives(t, 3)
+        blood(t, 3)
+        split(t, 1)
+        payload(t, 1, False)
+        sums(t, 2)
+
+    def moving_c(t):
+        feats(t, 3)
+        sums(t, 3, True)
+
+    def wed(t):
+        cnt = B + L * t
+        off = float(MID + t)
         kt = "K0" if t == 0 else "K"
-        key = "key%d" % (t % 2)
+        kwin = lambda n: V("K0", 0, n) if t == 0 else Kp(0, n)
         d = t % 3 + 1
         cm = lambda j: V("CM", 128 * j, 128 * j + 128)
-        sm = lambda j: V("sm", 16 * j, 16 * j + 16)
         ul = lambda j: V("uL", 16 * j, 16 * j + 16)
-        rep = V("repl")
         ac = 32 * d - 32 + 16 * (t // 3)
-        act(V("dS", L * t, L * t + L), IND(V(kt, 0, 2048), V("aR", ac, ac + 16)), AF.Copy, None, 512.0)
+        scale(V("dS", L * t, L * t + L), IND(kwin(2048), V("aR", ac, ac + 16)), 512.0)
         send(rank - d, V("dR", L * t, L * t + L), V("dS", L * t, L * t + L), "dq%d" % t, 8)
         if t < 2:
             asklists(t + 2)
@@ -463,136 +566,128 @@ def build(T, topo, core, rank):
         pcopy(V("pk"), xv(t))
         for nm, j in (("KW", 1), ("KW", 2), ("SW", 2)):
             pcopy(V(nm, j, 768, 3), kv)
-        for j in (1, 2):
-            pcopy(V("XW", j, 768, 3), xv(t))
         grp(V("pT3", 0, 256), [(V("CA", 128 * t, 128 * t + 128), V("kv16")), (w16(9 + t, 9 + t), V("J16"))])
         act(V("SW", 1, 768, 3), V("pT3", 0, 256), AF.Identity, col("BI", 24 + t))
-        scan(V("scn"), V("rst"), V(key), ALU.add, ALU.min)
-        cp(V("kI"), V("scn", 15, 512, 16))
-        ts(V("kJ"), V("kI"), 0x7F0000FF, ALU.bitwise_and)
-        for h in range(2):
-            ts(V("sm", 8 * h, 8 * h + 8), V("kJ", 16 * h, 16 * h + 8), 16.0, ALU.mult, 6144.0, ALU.min)
-            ts(V("sm", 16 + 8 * h, 24 + 8 * h), V("kJ", 16 * h + 8, 16 * h + 16), 255.0, ALU.min, -2056.0, ALU.add)
-        tt(V("mT"), sm(0), sm(1), ALU.add)
-        tt(V("LM"), IND(V("mT"), rep), V("Dm"), ALU.mult)
-        act(V("LR"), IND(V("mT"), rep))
-        for h in range(2):
-            tt(V("nk", 8 * h, 8 * h + 8), V("scn", 256 * h + 15, 256 * h + 128, 16), V("thz", 8 * h, 8 * h + 8), ALU.is_lt)
+        scan(V("scn", 512, 768), V("rst"), V("bD", 0, 256), ALU.max, ALU.min)
+        tt(V("F", 1, 64, 2), V("scn", 256 * (t % 2) + 7, 256 * (t % 2) + 256, 8), V("scn", 519, 768, 8), ALU.min)
+        ts(V("F", 0, 64, 2), V("F", 1, 64, 2), 256 * MAG0, ALU.add, 256 * MAG0, ALU.subtract)
+        scan(V("mT"), V("sd"), V("F"), ALU.mult, ALU.add)
+        act(V("LR"), IND(V("mT"), V("rep4")))
+        tt(V("LM"), IND(V("mT"), V("rep4")), V("Dm"), ALU.mult)
+        tt(V("nk"), V("F", 1, 64, 4), V("thz"), ALU.is_lt)
+        mm([(V("pT1", 128 * h, 128 * h + 128), V("LR", 128 * h, 128 * h + 128), IH, True, True) for h in range(2)])
         mm([(V("pT3", 256 + 8 * h, 264 + 8 * h), V("LM", 128 * h, 128 * h + 128), V("Blk16"), True, True) for h in range(2)])
-        mm([(V("pT1", 128 * h, 128 * h + 128), V("LR", 128 * h, 128 * h + 128), V("IH"), True, True) for h in range(2)])
-        mWp = V("pT3", 256, 272)
-        cp(V("mW"), mWp)
-        ts(ul(0), mWp, 2048.0, ALU.add, float(cnt - 1), ALU.min)
-        ts(sm(2), mWp, float(cnt - 1 - 2048), ALU.min, 2048.0 + EW - cnt, ALU.add)
-        cp(V("mR"), V("pT1", 0, 256))
-        mm([(V("pD2", 0, 256), V("Ib"), V("Mm"), True, False)]
-           + [(V("pD2", 128 * h, 128 * h + 128), V(nm, 128 * h, 128 * h + 128), V(rh), False, nm == "LM" and h == 1)
-              for nm, rh in (("LR", "IH"), ("LM", "nBR")) for h in range(2)])
+        mW = V("mW")
+        act(V("mR"), V("pT1", 0, 256))
+        ts(ul(0), V("pT3", 256, 272), off, ALU.add)
+        cp(mW, V("pT3", 256, 272))
+        mm([(V("pX1", 0, 256), V("Ib"), V("Mm"), True, False)]
+           + [(V("pX1", 128 * h, 128 * h + 128), V(nm, 128 * h, 128 * h + 128), rh, False, nm == "LM" and h == 1)
+              for nm, rh in (("LR", IH), ("LM", V("nBR"))) for h in range(2)])
+        act(V("km"), IND(kwin(cnt), ul(0)), AF.Identity, col("BI", 16 + t), col("pF", 15))
         act(V("xm"), IND(V("X", 0, cnt), ul(0)))
         cP = lambda h: V("pT2", 8 * h, 8 * h + 8)
         Eh = lambda s, h: V("E", 256 * s + 128 * h, 256 * s + 128 * h + 128)
-        b1 = V("RR", 56, 64)
+        b1 = V("Blkb")
         mm([(V("pT2", 0, 16), V("nIb"), V("nk"), True, False)])
+        ts(V("E", 256 * 15, 256 * 16), V("pX1", 0, 256), 0.0, ALU.is_equal)
+        mm([(cP(h), Eh(15, h), b1, False, False) for h in range(2)])
         for s in range(15):
             ts(V("E", 256 * s + 16 * s + 16, 256 * s + 256), V("mR", 16 * s + 16, 256), col("mW", s), ALU.is_equal)
             if s % 3 == 2:
-                mm([(cP(h), Eh(u, h), b1, False, False) for u in range(s - 2, s + 1) for h in range(2) if h == 1 or u < 7])
-        ts(V("E", 256 * 15, 256 * 16), V("pD2", 0, 256), 0.0, ALU.is_equal)
-        mm([(cP(h), Eh(15, h), b1, False, h == 1) for h in range(2)])
-        if ACT16:
-            act(V("km16"), IND(V(kt, 0, cnt), ul(0)), AF.Copy, -2048.0)
-        else:
-            ts(V("km16"), IND(V(kt, 0, cnt), ul(0)), -2048.0, ALU.add)
+                mm([(cP(h), Eh(u, h), b1, False, u == 14) for u in range(s - 2, s + 1) for h in range(2) if h == 1 or u < 7])
+        act(V("MZ", 0, 16), mW, AF.Copy, off + PAD)
         eP = V("pT1", 256, 304)
-        mm([(eP, I32v, V("CE", 0, 48), True, False)])
+        mm([(eP, V("I32"), V("CE", 0, 48), True, False)])
         ts(V("lost"), V("pT2", 0, 16), 0.0, ALU.is_ge)
-        tt(V("Lw"), IND(V("lost"), rep), V("wt"), ALU.mult)
-        act(V("Lr"), IND(V("lost"), rep))
+        tt(V("Lw"), IND(V("lost"), V("repl")), V("wt"), ALU.mult)
+        act(V("Lr"), IND(V("lost"), V("repl")))
         grp(eP, [(V(nm, 128 * h, 128 * h + 128), V("RE", o + 48 * h, o + 48 * h + 48))
                  for nm, o in (("Lw", 0), ("Lr", 96)) for h in range(2)], False, True)
-        grp(V("pD2", 0, 256), [(cm(3), V("kv16")), (w16(7, 7), V("J16")), (w16(6, 6), V("mR"))])
-        act(V("SW", 0, 768, 3), V("pD2", 0, 256), AF.Identity, col("BI", 8 + t))
-        grp(V("pD1", 0, 256), [(cm(4), V("J16")), (cm(3), V("km16"))])
-        act(V("kmN"), V("pD1", 0, 256), AF.Identity, col("BI", 16 + t))
-        grp(V("pD2", 256, 512), [(cm(0), V("kv16")), (cm(2), V("J16")), (w16(1, 1), V("mR")), (cm(1), V("km16"))])
-        act(V("KW", 0, 768, 3), V("pD2", 256, 512), AF.Identity, col("BI", t))
-        grp(V("pT3", 0, 256), [(V("oneb", p=one), V("qc", p=one)), (V("hIb"), xv(t)), (V("hIb"), V("xm"))])
-        ts(V("XW", 0, 768, 3), V("pT3", 0, 256), MAG0, ALU.add, MAG0, ALU.subtract)
-        ts(ul(1), V("pT1", 256, 272), MAG0, ALU.add, MAG0, ALU.subtract)
-        tt(sm(3), V("pT1", 272, 288), sm(2), ALU.max)
-        ts(sm(4), V("pT1", 272, 288), -EW, ALU.add)
-        ts(ul(2), sm(3), cnt - EW, ALU.add)
-        tt(sm(5), V("pT1", 288, 304), sm(4), ALU.max)
-        ts(sm(6), V("pT1", 256, 272), MAG0, ALU.add, MAG0, ALU.subtract)
-        cp(ul(3), sm(5))
-        cp(IND(V("K", 0, cnt + L), ul(2)), V("kmN"))
-        act(lanes("K", t), IND(V("SW"), ul(1)))
-        act(V("K", cnt, cnt + L), IND(V("KW"), ul(1)))
+        grp(V("pX2", 0, 256), [(cm(2), V("kv16")), (w16(7, 7), V("J16")), (w16(6, 6), V("mR"))])
+        act(V("SW", 0, 768, 3), V("pX2", 0, 256), AF.Identity, col("BI", 8 + t))
+        grp(V("pX2", 256, 512), [(cm(0), V("kv16")), (cm(1), V("J16")), (w16(1, 1), V("mR")), (V("CM32"), V("km"))])
+        act(V("KW", 0, 768, 3), V("pX2", 256, 512), AF.Identity, col("BI", t))
+        grp(V("pT3", 0, 256), [(ones, V("qc", 0, 256, p=one)), (V("hIb"), xv(t)), (V("hIb"), V("xm"))])
         if t < R - 1:
-            kbcopy("K", cnt, cnt + L)
+            ts(V("X", cnt, cnt + L), V("pT3", 0, 256), MAG0, ALU.add, MAG0, ALU.subtract)
+            dma([(T.XW[:, 256:512], T.X[:, cnt:cnt + L])], [("X", cnt, cnt + L)], [("XW", 256, 512)], 65536)
+        else:
+            ts(V("XW", 256, 512), V("pT3", 0, 256), MAG0, ALU.add, MAG0, ALU.subtract)
+        tt(V("zz"), V("pT1", 272, 304), V("MZ"), ALU.min)
+        cp(V("uL", 32, 64), V("zz"))
+        ts(ul(1), V("pT1", 256, 272), MAG0, ALU.add, MAG0, ALU.subtract)
         tt(IND(V("pc"), ul(3)), V("dR", L * t, L * t + L), V("pk"), ALU.add)
-        ts(V("dU"), V("pc", 0, 64), 1.0 / 512, ALU.mult)
-        ts(V("pr"), V("pc", 0, 64), 512 * MAG0, ALU.add, 512 * MAG0, ALU.subtract)
-        tt(V("xc"), V("pc", 0, 64), V("pr"), ALU.subtract)
+        act(lanes("K", t), IND(V("SW"), ul(1)))
+        act(Kp(cnt, cnt + L), IND(V("KW"), ul(1)))
+        tt(IND(V("K", 0, PAD + cnt), ul(2)), V("km"), V("VN"), ALU.add)
+        if t < R - 1:
+            kbcopy("K", PAD, cnt, cnt + L)
+        pairs = [(yk[:, cnt:cnt + L], T.K[:, PAD + cnt:PAD + cnt + L]),
+                 (yk[9 + t:128:16, 0:2048], T.K[9 + t:128:16, PAD:PAD + 2048])]
+        nb = 128 * 1024 + 65536
+        if t == R - 1:
+            pairs += [(yk[r:128:16, 0:cnt], T.K[r:128:16, PAD:PAD + cnt]) for r in (6, 7)]
+            nb += 16 * cnt * 4
+        dma(pairs, [("K", 0, PAD + cnt + L)], [("yk", 0, W)], nb)
+
+    def ask(t):
+        cnt = B + L * t
+        d = t % 3 + 1
+        ts(V("dU"), V("pc", 192, 256), 1.0 / 512, ALU.mult)
+        ts(V("pr"), V("pc", 192, 256), 512 * MAG0, ALU.add, 512 * MAG0, ALU.subtract)
+        tt(V("xc"), V("pc", 192, 256), V("pr"), ALU.subtract)
         for c in range(2):
-            (cp if c == 1 and t == R - 1 else act)(V("Xa", 512 * c, 512 * c + 512),
-                                                   IND(V("XQ%d" % d, 0, cnt), V("dU", 32 * c, 32 * c + 32)))
+            (act if CFG["XA"][t][c] == "a" else cp)(V("Xa", 512 * c, 512 * c + 512),
+                                                    IND(V("XQ%d" % d, 0, cnt), V("dU", 32 * c, 32 * c + 32)))
         lo = (0, 64)
-        mm([(V("pT2", 0, 128, p=lo), V("one16", 0, 64, p=one), V("kca", p=one), True, False)])
+        mm([(V("pT2", 0, 128, p=lo), V("oneb", 0, 64, p=one), V("kca", p=one), True, False)])
         for c in range(2):
             bank = ("pT3", "pT1")[c]
             mm([x for k in range(8 * c, 8 * c + 8) for x in
                 ((V(bank, 64 * (k % 8), 64 * (k % 8) + 64), V("Ib"), V("Xa", k, 1024, 16), True, False),
                  (V(bank, 64 * (k % 8), 64 * (k % 8) + 64), V("nIb"), V("xc"), False, True))])
             act(V("Da", 512 * c, 512 * c + 512), V(bank), AF.Abs)
-            mm([(V("pT2", k, 128, 16, p=lo), V("Da", 64 * k, 64 * k + 64), V("RR", 48, 56), False, k == 15)
+            mm([(V("pT2", k, 128, 16, p=lo), V("Da", 64 * k, 64 * k + 64), V("RR", 64, 72), False, k == 15)
                 for k in range(8 * c, 8 * c + 8)])
-        ts(sm(7), sm(4), 768.0, ALU.add)
-        ts(sm(8), sm(4), 64.0, ALU.is_lt, 4096.0, ALU.mult)
-        tt(sm(7), sm(7), sm(8), ALU.min)
-        tt(sm(7), sm(7), sm(6), ALU.max)
-        cp(ul(4), sm(7))
-        scan(V("asn", p=lo), V("rst", 0, 128, p=lo), V("pT2", 0, 128, p=lo), ALU.add, ALU.min)
+        ts(V("pT3", 0, 192), V("pc", 0, 192), 512 * MAG0, ALU.add, 512 * MAG0, ALU.subtract)
+        tt(V("XW", 0, 192), V("pc", 0, 192), V("pT3", 0, 192), ALU.subtract)
+        if t < R - 1:
+            grp(V("pT1", 0, 16), [(V("o4k", p=one), V("qc", 256, 272, p=one)), (V("o4k"), V("lost"))])
+            add("dve", lambda g: g.vector.tensor_reduce(T.zF[:, 0:1], T.pT1[:, 0:16], AX.X, ALU.add),
+                [("pT1", 0, 16)], [("zF", 0, 1)], (16, 64, 0, 0, 0, 0))
+            ts(col("zF", 1), col("zF", 0), 65536 * MAG0, ALU.add, 65536 * MAG0, ALU.subtract)
+            for h in range(2):
+                ts(V("thz", 8 * h, 8 * h + 8), V("thB", t + 1, 48, 6), col("zF", 1), ALU.add, col("zF", 0), ALU.subtract)
+        scan(V("asn", p=lo), V("rsa", p=lo), V("pT2", 0, 128, p=lo), ALU.add, ALU.min)
         cp(V("bI", p=lo), V("asn", 15, 128, 16, p=lo))
         ts(V("bJ", p=lo), V("bI", p=lo), 15, ALU.bitwise_and)
         tt(V("bL"), IND(V("bJ"), V("repl", 0, 8)), V("Dm", 0, 128), ALU.mult)
-        grp(V("pT2", 256, 260), [(I32v, V("CE", 48, 52)), (V("bL", p=lo), V("Blk16", 0, 4, p=lo))])
-        cp(V("uL", 80, 84), V("pT2", 256, 260))
-        act(V("XW", 768, 832), IND(V("Xa"), V("uL", 80, 84)))
-        act(V("X", cnt, cnt + L), IND(V("XW"), ul(4)))
+        grp(V("pT2", 256, 260), [(V("I32"), V("CE", 48, 52)), (V("bL", p=lo), V("Blk16", 0, 4, p=lo))])
+        cp(V("uL", 64, 68), V("pT2", 256, 260))
+        act(V("XW", 192, 256), IND(V("Xa"), V("uL", 64, 68)))
+        act(V("X", cnt, cnt + L), IND(V("XW"), V("uL", 48, 64)))
         for u, dd in sorted(XSEND, key=lambda x: (x[1] - (t + 1) % 3 - 1) % 3):
             if u == t:
                 send(rank - dd, V("XQ%d" % dd, cnt, cnt + L), V("X", cnt, cnt + L), "xn%d_%d" % (u, dd), 8)
-        if t < R - 1:
-            grp(V("pT3", 0, 16), [(V("oneb"), V("Lr", 0, 256, 16))])
-            add("dve", lambda g: g.vector.tensor_reduce(T.zF[:, 0:1], T.pT3[:, 0:16], AX.X, ALU.add),
-                [("pT3", 0, 16)], [("zF", 0, 1)], 90.0)
-            ts(col("zI", 0), col("zF", 0), -1.0, ALU.mult, 2048.0, ALU.add)
-            ts(col("zI", 1), col("zI", 0), 15, ALU.bitwise_and)
-            ts(col("zF", 1), col("zI", 1), 4096.0, ALU.mult)
-            for h in range(2):
-                ts(V("thz", 8 * h, 8 * h + 8), V("thB", t + 1, 48, 6), col("zF", 1), ALU.add, BIG, ALU.min)
-        pairs = [(yk[:, cnt:cnt + L], T.K[:, cnt:cnt + L]), (yk[9 + t:128:16, 0:2048], T.K[9 + t:128:16, 0:2048])]
-        nb = 128 * 1024 + 65536
-        if t == R - 1:
-            pairs += [(yk[r:128:16, 0:cnt], T.K[r:128:16, 0:cnt]) for r in (6, 7)]
-            nb += 16 * cnt * 4
-        dma(pairs, [("K", 0, cnt + L)], [("yk", 0, W)], nb)
         dma([(yx[:, L * t:L * t + L], T.X[:, cnt:cnt + L])], [("X", cnt, cnt + L)], [("yx", L * t, L * t + L)], 65536)
 
-    spread("kvb0", "KB", 0)
-    spread("xvb0", "X", 0)
-    batch(0, "S")
+    spreads(0)
+    still(0)
     late_constants()
+    moving_a(0)
+    moving_b(0)
+    dma([(yk[:, 0:B], T.K0[:])], [("K0", 0, B), ("eq", 5120, 5632)], [("yk", 0, W)], 128 * B * 4)
     for t in range(R):
-        batch(t, "D")
-        if t == 0:
-            dma([(yk[:, 0:B], T.K0[:])], [("K0", 0, B), ("eqD", 0, 512)], [("yk", 0, W)], 128 * B * 4)
+        moving_c(t)
         if t + 1 < R:
-            spread("kvb%d" % ((t + 1) % 2), "KB", t + 1)
-            spread("xvb%d" % ((t + 1) % 2), "X", t + 1)
-            batch(t + 1, "S")
-        tail(t)
+            spreads(t + 1)
+            still(t + 1)
+        wed(t)
+        if t + 1 < R:
+            moving_a(t + 1)
+            moving_b(t + 1)
+        ask(t)
     return ops
 
 
@@ -609,7 +704,7 @@ def depend(ops):
                 if j == o["id"]:
                     continue
                 if name in PS:
-                    dep[j] = dep.get(j, False) or ops[j]["eng"] != o["eng"]
+                    dep[j] = dep.get(j, False) or ops[j]["eng"] != o["eng"] or (o["eng"] != "pe" and (w or w2))
                 elif (w or w2) and a < b2 and a2 < b and (st != st2 or (a - a2) % st == 0):
                     dep[j] = True
         for name, a, b, st, w in acc:
@@ -623,57 +718,18 @@ def depend(ops):
         o["dep"] = dep
 
 
-def schedule(ops):
-    n = len(ops)
-    succ = [[] for _ in range(n)]
-    for o in ops:
-        for j in o["dep"]:
-            succ[j].append(o["id"])
-    dur = [o["cost"] + o.get("lat", 0.0) for o in ops]
-    prio = [0.0] * n
-    for i in range(n - 1, -1, -1):
-        prio[i] = dur[i] + max([prio[k] + (HOP if ops[k]["dep"][i] else 0.0) for k in succ[i]] + [0.0])
-    left = [len(o["dep"]) for o in ops]
-    ready = [i for i in range(n) if left[i] == 0]
-    rdy = [0.0] * n
-    free = {}
-    order = []
-    while ready:
-        est = {i: max(rdy[i], free.get(ops[i]["eng"], 0.0)) for i in ready}
-        i0 = min(ready, key=lambda i: (est[i], -prio[i]))
-        e = ops[i0]["eng"]
-        pick = i0
-        if e != "recv":
-            for i in ready:
-                if ops[i]["eng"] == e and prio[i] > prio[pick] and est[i] < est[i0] + 0.5 * ops[i0]["cost"]:
-                    pick = i
-        o = ops[pick]
-        o["t0"] = est[pick]
-        if e != "recv":
-            free[e] = est[pick] + o["cost"]
-        o["t1"] = est[pick] + dur[pick]
-        order.append(pick)
-        ready.remove(pick)
-        for k in succ[pick]:
-            rdy[k] = max(rdy[k], o["t1"] + (HOP if ops[k]["dep"][pick] else 0.0))
-            left[k] -= 1
-            if left[k] == 0:
-                ready.append(k)
-    return order
-
-
-def place(ops, seq, pred, back):
+def place(ops, cost, hop, seq, pred, back):
     t0 = [0.0] * len(ops)
     gaps = {e: [[0.0, 1e12]] for e in ENG}
     end = 0.0
     for i in seq:
         o = ops[i]
-        c, lat = o["cost"], o.get("lat", 0.0)
+        c, lat = cost[i], o.get("lat", 0.0)
         r = lat if back else 0.0
         for j, hard in pred[i]:
-            x = t0[j] + ops[j]["cost"]
+            x = t0[j] + cost[j]
             if hard:
-                x += HOP + (lat if back else ops[j].get("lat", 0.0))
+                x += hop + (lat if back else ops[j].get("lat", 0.0))
             r = max(r, x)
         if o["eng"] != "recv":
             gl = gaps[o["eng"]]
@@ -690,17 +746,35 @@ def place(ops, seq, pred, back):
     return t0, end
 
 
-SHAKE = 3000.0
+def replay(ops, cost, hop, order, pred):
+    free = {}
+    t1 = [0.0] * len(ops)
+    for i in order:
+        e = ops[i]["eng"]
+        r = free.get(e, 0.0)
+        for j, hard in pred[i]:
+            if hard and t1[j] + hop > r:
+                r = t1[j] + hop
+        if e != "recv":
+            free[e] = r + cost[i]
+        t1[i] = r + cost[i] + ops[i].get("lat", 0.0)
+    return max(t1)
 
 
-def improve(ops, rounds=400):
+def improve(ops, rounds=300):
     n = len(ops)
     pred = [list(o["dep"].items()) for o in ops]
     succ = [[] for _ in range(n)]
     for o in ops:
         for j, hard in o["dep"].items():
             succ[j].append((o["id"], hard))
-    seq = schedule(ops)
+    cost = [price(o, NOMINAL) for o in ops]
+    hop = NOMINAL[4]
+    more = [([price(o, m) for o in ops], m[4], m[0]) for m in OTHERS]
+    prio = [0.0] * n
+    for i in range(n - 1, -1, -1):
+        prio[i] = cost[i] + ops[i].get("lat", 0.0) + max([prio[k] + (hop if h else 0.0) for k, h in succ[i]] + [1e-3])
+    seq = sorted(range(n), key=lambda i: (-prio[i], i))
     best = None
     x = [12345]
 
@@ -708,40 +782,66 @@ def improve(ops, rounds=400):
         x[0] = (x[0] * 1103515245 + 12345) % 2147483648
         return x[0] / 2147483648.0
     for it in range(rounds):
-        t0, end = place(ops, seq, pred, False)
-        if best is None or end < best[0]:
-            best = (end, t0)
+        t0, end = place(ops, cost, hop, seq, pred, False)
+        if best is None or end < best[2] * 1.02:
+            order = sorted(range(n), key=lambda i: (t0[i], i))
+            val = end / NOMINAL[0] + sum(replay(ops, c, h, order, pred) / f for c, h, f in more)
+            if best is None or val < best[0]:
+                best = (val, t0, end, order)
         if it % 4 == 3:
-            lo = rnd() * best[0]
+            lo = rnd() * best[2]
             key = [0.0] * n
             for i in range(n):
                 k = best[1][i]
                 if lo <= k < lo + 30000.0:
-                    k += (rnd() - 0.5) * SHAKE
+                    k += (rnd() - 0.5) * 3000.0
                 key[i] = max([k] + [key[j] + 1e-3 for j, _h in pred[i]])
             seq = sorted(range(n), key=lambda i: (key[i], i))
             continue
-        seq = sorted(range(n), key=lambda i: (-(t0[i] + ops[i]["cost"] + ops[i].get("lat", 0.0)), -i))
-        tb, _e = place(ops, seq, succ, True)
-        seq = sorted(range(n), key=lambda i: (-(tb[i] + ops[i]["cost"]), i))
+        seq = sorted(range(n), key=lambda i: (-(t0[i] + cost[i] + ops[i].get("lat", 0.0)), -i))
+        tb, _e = place(ops, cost, hop, seq, succ, True)
+        seq = sorted(range(n), key=lambda i: (-(tb[i] + cost[i]), i))
     for o in ops:
         o["t0"] = best[1][o["id"]]
-        o["t1"] = o["t0"] + o["cost"] + o.get("lat", 0.0)
-    return sorted(range(n), key=lambda i: (best[1][i], i))
+        o["t1"] = o["t0"] + cost[o["id"]] + o.get("lat", 0.0)
+    return best[3]
 
 
 ORDER = {}
 
 
-def rank_program(g, core, T, topo):
-    rank = T.rank_of(core)
-    if rank is None:
-        return
+def ordered(T, topo, core, rank):
     ops = build(T, topo, core, rank)
     depend(ops)
     if "all" not in ORDER:
         ORDER["all"] = improve(ops)
-    order = ORDER["all"]
+    return ops, ORDER["all"]
+
+
+def hand_back(g, core, T, topo, rank):
+    dst = T.cores[rank]
+    rid, pid = topo.addr(dst)[:2]
+    sent = 0
+    for t in range(R):
+        for p in range(2):
+            if CFG["XR"][t][2 * p] in "fg":
+                tag = "%d_%d" % (t, p)
+                blk = T.Mx[:, 2048 * t + 1024 * p:2048 * t + 1024 * p + 1024]
+                g.wait_ge(T.sem["fo" + tag], 16)
+                g.remote_dma(blk, blk, T.sem["fb" + tag], T.sem.sent, pid, rid, mask_of(topo, core, dst, 16))
+                sent += 16
+    if sent:
+        g.wait_ge(T.sem.sent, sent)
+
+
+def rank_program(g, core, T, topo):
+    rank = T.rank_of(core)
+    if rank is None:
+        for r, c in enumerate(T.cores):
+            if core in topo.cores_of(c) and helper_of(T, topo, c) == core:
+                hand_back(g, core, T, topo, r)
+        return
+    ops, order = ordered(T, topo, core, rank)
     queue = {"pe": g.tensor, "dve": g.vector, "act": g.scalar, "pool": g, "sp": g.sync}
     needed = set(j for o in ops for j, hard in o["dep"].items() if hard)
     count = {e: 0 for e in ENG}

from concourse.bass import DstId, RemoteDMATransfer
from concourse.mybir import AluOpType as ALU, AxisListType as AX, ActivationFunctionType as AF

N, R, L, B, W = 4, 6, 256, 2304, 3840
F32, BF, F16, I32, U16 = "float32", "bfloat16", "float16", "int32", "uint16"
SZ = {F32: 4, BF: 2, F16: 2, I32: 4, U16: 2}
EW = 8128.0
MAG0 = 12582912.0
BIG = 33554432.0
MID = 1920
PAD = 256

CFG = {
    "KG": ["avavaaav"] + ["aaaaaaav"] * 5,
    "XR": ["ffffaaad"] * 6,
    "XA": ["av"] * 6,
    "SP0": "ppppvvvv",
}

SB = {
    "kint": ([128, B], I32), "K0": ([128, B], F32), "K": ([128, PAD + W], F32), "KB": ([128, W], F32),
    "X": ([128, W], BF), "XQ1": ([128, W - L], BF), "XQ2": ([128, W - L], BF), "XQ3": ([128, W - L], BF),
    "kvb0": ([128, 1024], F32), "kvb1": ([128, 1024], F32), "xvb0": ([128, 1024], BF), "xvb1": ([128, 1024], BF),
    "G16": ([128, 4096], F16), "Xc": ([128, 6144], BF), "Dab": ([128, 4096], BF), "eq": ([128, 6144], BF),
    "Mx": ([128, R * 2048], BF), "l1": ([128, 512], U16), "l2": ([128, 256], U16), "hi": ([128, 384], BF), "lo": ([128, 384], BF),
    "mW": ([128, 16], F32),
    "pI": ([128, 8], I32), "pF": ([128, 32], F32), "J": ([128, 256], F32), "JB": ([128, 256], F32),
    "J16": ([128, 256], F16), "RM": ([128, 16], F32), "Blk": ([128, 8], F32), "Blk16": ([128, 8], F16), "Blkb": ([128, 8], BF),
    "IW": ([128, 176], F16), "I32": ([128, 128], F32), "MP": ([128, 4 * 176], F16), "W16": ([128, 16 * 144], F16),
    "SEL": ([128, 128], F16), "Ib": ([128, 128], BF), "nIb": ([128, 128], BF), "hIb": ([128, 128], BF), "o4k": ([128, 128], BF),
    "Dm": ([128, 256], BF), "wt": ([128, 256], F32), "Mm": ([128, 256], BF), "repl": ([128, 16], U16), "rep4": ([128, 16], U16),
    "RR": ([128, 80], BF), "RX": ([128, 128], BF), "RE": ([128, 192], BF), "CE": ([128, 64], F32), "tmpc": ([128, 256], F32),
    "I16": ([128, 128], BF), "kc": ([128, 512], BF), "oneb": ([128, 128], BF), "kca": ([128, 128], BF),
    "qc": ([128, 272], BF), "CM": ([128, 3 * 128], F16), "CM32": ([128, 128], F32), "CA": ([128, 6 * 128], F16),
    "BI": ([128, 32], F32), "VN": ([128, 256], F32),
    "wI": ([128, 8], I32), "wF": ([128, 8], F32), "wS": ([128, 48], BF), "thI": ([128, 48], I32), "thF": ([128, 48], F32),
    "thB": ([128, 48], F32), "thz": ([128, 16], F32), "zF": ([128, 32], F32),
    "aI": ([128, 96], I32), "aJ": ([128, 96], I32), "aL": ([128, 256], F16), "aU": ([128, 96], U16),
    "aR": ([128, 96], U16), "dS": ([128, R * L], F32), "dR": ([128, R * L], F32),
    "scn": ([128, 768], F32), "rst": ([128, 256], F32), "rsa": ([128, 128], F32), "sd": ([128, 64], F32),
    "F": ([128, 64], F32), "mT": ([128, 64], F32), "nk": ([128, 16], BF), "MZ": ([128, 32], F32), "zz": ([128, 32], F32),
    "lost": ([128, 16], BF), "LM": ([128, 256], F16), "LR": ([128, 256], F16),
    "mR": ([128, 256], F16), "E": ([128, 16 * 256], BF), "Lw": ([128, 256], BF), "Lr": ([128, 256], BF),
    "uL": ([128, 80], U16), "kv16": ([128, 256], F16), "ks16": ([128, 256], F16), "km": ([128, 256], F32), "xm": ([128, 256], BF),
    "KW": ([128, 768], F32), "SW": ([128, 768], F32), "XW": ([128, 512], BF),
    "pk": ([128, 256], F32), "pc": ([128, 512], F32), "pr": ([128, 64], F32), "xc": ([128, 64], BF), "dU": ([128, 64], U16),
    "Xa": ([128, 1024], BF), "Da": ([128, 1024], BF), "asn": ([128, 128], F32), "bI": ([128, 8], I32), "bJ": ([128, 8], I32),
    "bL": ([128, 128], F16), "nBR": ([128, 128], F16),
}
PS = ["bS", "bD", "pX1", "pX2", "pT1", "pT2", "pT3", "bF"]
SCRATCH = {k: ("sbuf", v[0], v[1]) for k, v in SB.items()}
for _p in PS:
    SCRATCH[_p] = ("psum", [128, 512], F32)

ENG = ["pe", "dve", "act", "pool", "sp"]
XSEND = [(u, d) for u in range(R - 1) for d in (1, 2, 3) if any(t % 3 + 1 == d for t in range(u + 1, R))]
SEMAPHORES = (["c_" + e for e in ENG[:4]] + ["d%d" % i for i in range(48)] + ["sent"] + ["xi%d" % d for d in (1, 2, 3)]
              + ["al%d" % d for d in (1, 2, 3)] + ["dq%d" % t for t in range(R)] + ["xn%d_%d" % ud for ud in XSEND]
              + ["%s%d_%d" % (s, t, p) for s in ("fo", "fb") for t in range(R) for p in range(2)])

NOMINAL = (1.15, 1.56, 3.8, 0.42, 150.0, 500.0)
OTHERS = [(1.0, 1.56, 3.8, 0.42, 150.0, 400.0), (1.1, 1.15, 2.5, 0.42, 150.0, 600.0), (1.4, 1.9, 5.0, 0.42, 150.0, 600.0),
          (1.25, 1.3, 5.0, 0.42, 200.0, 800.0)]


def price(o, m):
    fix, cyc, ga, sc, pe, raw = o["c"]
    return m[0] * (fix + 0.83 * (cyc + ga * m[1] + sc * m[2]) + pe * m[3]) + raw + (m[5] if "rem" in o else 0.0)


def helper_of(T, topo, core):
    same = [c for c in topo.cores_of(core) if topo.die(c) == topo.die(core)]
    return [c for c in same if c not in T.cores][[c for c in same if c in T.cores].index(core)]


def mask_of(topo, src, dst, ne):
    mask = 0
    for e in topo.engines(src, dst)[:ne]:
        mask |= 1 << e
    return mask


def build(T, topo, core, rank):
    ops = []

    def V(name, c0=None, c1=None, st=None, p=None):
        ncol = 512 if name in PS else SB[name][0][1]
        a = 0 if c0 is None else c0
        b = ncol if c1 is None else c1
        ps = slice(None) if p is None else slice(*p)
        cs = slice(a, b) if st is None else slice(a, b, st)
        n = len(range(a, b, st or 1))
        w = 4 if name in PS else SZ[SB[name][1]]
        return {"ap": T[name][ps, cs], "reg": [(name, a, b, st or 1)], "n": n, "w": w, "ps": name in PS}

    def IND(win, off):
        return {"ap": win["ap"].indirect(off["ap"]), "reg": win["reg"] + off["reg"], "n": 16 * off["n"], "w": 4,
                "ps": False, "ind": True, "off": off["reg"], "win": win["reg"]}

    def ap(x):
        return x["ap"] if isinstance(x, dict) else x

    def regs(xs):
        r = []
        for x in xs:
            if isinstance(x, dict):
                r += x["reg"]
        return r

    def add(eng, fn, rd, wr, c, **kw):
        o = {"eng": eng, "fn": fn, "rd": rd, "wr": wr, "c": c, "id": len(ops)}
        o.update(kw)
        ops.append(o)
        return o

    def vcost(out, ins, two):
        if out.get("ind"):
            return (40, 0, 0, out["n"], 0, 0)
        if ins[0].get("ind"):
            return (40, 0, out["n"], 0, 0, 0)
        f = 1.0
        if two and not any(x["ps"] for x in ins):
            f = 2.0
        elif not two and out["w"] == 2 and all(x["w"] == 2 for x in ins):
            f = 0.5
        return (16, max(64, out["n"] * f), 0, 0, 0, 0)

    def vadd(fn, out, ins, extra, two):
        rd = regs(ins + extra)
        wr = out["reg"]
        if out.get("ind"):
            rd = rd + out["off"]
            wr = out["win"]
        return add("dve", fn, rd, wr, vcost(out, ins, two))

    def cp(out, a):
        vadd(lambda g: g.vector.tensor_copy(out["ap"], a["ap"]), out, [a], [], False)

    def ts(out, a, s1, o1, s2=None, o2=None):
        if o2 is None:
            vadd(lambda g: g.vector.tensor_scalar(out["ap"], a["ap"], ap(s1), None, o1), out, [a], [s1], False)
        else:
            vadd(lambda g: g.vector.tensor_scalar(out["ap"], a["ap"], ap(s1), ap(s2), o1, o2), out, [a], [s1, s2], False)

    def tt(out, a, b, o):
        vadd(lambda g: g.vector.tensor_tensor(out["ap"], a["ap"], b["ap"], o), out, [a, b], [], True)

    def scan(out, d0, d1, o0, o1):
        vadd(lambda g: g.vector.tensor_tensor_scan(out["ap"], d0["ap"], d1["ap"], 0.0, o0, o1), out, [d0, d1], [], False)

    def ms(out, c):
        vadd(lambda g: g.vector.memset(out["ap"], c), out, [out], [], False)
        ops[-1]["rd"] = []

    def act(out, a, func=AF.Copy, bias=None, scale=None):
        kw = {}
        if bias is not None:
            kw["bias"] = ap(bias)
        if scale is not None:
            kw["scale"] = ap(scale)
        c = (52, 0, out["n"], 0, 0, 0) if a.get("ind") else (52, out["n"], 0, 0, 0, 0)
        add("act", lambda g: g.scalar.activation(out["ap"], a["ap"], func, **kw), regs([a, bias, scale]), out["reg"], c)

    def scale(out, a, s):
        act(out, a, AF.Copy, None, s)

    def shifted(q, out, a, c):
        if q == "a":
            act(out, a, AF.Copy, c)
        else:
            ts(out, a, c, ALU.add)

    def mm(items):
        def fn(g):
            ins = None
            for o, l, r, s0, s1 in items:
                ins = g.tensor.matmul(o["ap"], l["ap"], r["ap"], s0, s1)
            return ins
        c = 0
        rd, wr = [], []
        for o, l, r, s0, s1 in items:
            c += max(min(64, l["n"]), r["n"]) * (4 if r["w"] == 4 else 1)
            rd += l["reg"] + r["reg"]
            wr += o["reg"]
        add("pe", fn, rd, wr, (24, 0, 0, 0, c, 0))

    def grp(out, pairs, first=True, last=True):
        mm([(out, l, r, first and i == 0, last and i == len(pairs) - 1) for i, (l, r) in enumerate(pairs)])

    def iota(out, pat, base=0, cm=0, fl=True):
        kw = {"allow_small_or_imprecise_dtypes": True} if fl else {}
        add("pool", lambda g: g.iota(out["ap"], pat, base, cm, **kw), [], out["reg"], (130, 2 * out["n"], 0, 0, 0, 0))

    def psel(out, a, pat, base):
        add("pool", lambda g: g.affine_select(out["ap"], a["ap"], pat, ALU.is_ge, 0.0, base, 0),
            a["reg"], out["reg"], (170, 2 * out["n"], 0, 0, 0, 0))

    def pcopy(out, a):
        psel(out, a, [[0, out["n"]]], 1)

    nd = [0]

    def dma(pairs, rd, wr, nbytes, q="sp"):
        sem = "d%d" % nd[0]
        nd[0] += 1

        def fn(g):
            e = g.sync if q == "sp" else g.scalar
            for o, i in pairs:
                e.dma_start(o, i).then_inc(T.sem[sem], 16)
            return None
        add(q, fn, rd, wr, (0, 0, 0, 0, 0, 60.0 * len(pairs)), lat=1800 + nbytes / 150.0, sem=sem, cnt=16 * len(pairs))

    def send(dst_rank, out, a, sem, ne=16):
        dst = T.cores[dst_rank % N]
        rid, pid = topo.addr(dst)[:2]
        mask = mask_of(topo, core, dst, ne)
        o = add("pool", lambda g: g.remote_dma(out["ap"], a["ap"], T.sem[sem], T.sem.sent, pid, rid, mask),
                a["reg"], [], (0, 0, 0, 0, 0, 0), rem=ne)
        add("recv", None, [], out["reg"], (0, 0, 0, 0, 0, 0), lat=2500 + 128 * a["n"] * a["w"] / 120.0, sem=sem, cnt=ne,
            after=o["id"])

    def fold(out, a, b, tag):
        dst = helper_of(T, topo, core)
        rid, pid = topo.addr(dst)[:2]
        mask = mask_of(topo, core, dst, 16)

        def fn(g):
            tr = RemoteDMATransfer(dst_ids=[DstId(rid=rid, pnc=pid)], dma_engine_mask=mask, remote_sem=T.sem["fo" + tag],
                                   srcs=[a["ap"], b["ap"]], dsts=[out["ap"]], alu_op=2)
            return g.remote_dma_fused([tr], local_sem=T.sem["fb" + tag])
        o = add("pool", fn, a["reg"] + b["reg"], [("folds", 0, 1)], (0, 0, 0, 0, 0, 0), rem=0)
        add("recv", None, a["reg"] + b["reg"], out["reg"], (0, 0, 0, 0, 0, 0), lat=5000 + 3 * 128 * a["n"] * a["w"] / 200.0,
            sem="fb" + tag, cnt=32, after=o["id"])

    yk, yx = T.yk, T.yx
    col = lambda name, j: V(name, j, j + 1)
    one = (0, 1)
    Kp = lambda c0, c1, st=None: V("K", PAD + c0, PAD + c1, st)

    qb = B // 4
    for q in range(4):
        dma([(T.kint[:, qb * q:qb * q + qb], T.kin[:, qb * q:qb * q + qb])], [], [("kint", qb * q, qb * q + qb)],
            128 * qb * 4 * (q + 1) * 0.6, q=("sp", "act")[q % 2])
    dma([(T.X[:, 0:B], T.xf[:])], [], [("X", 0, B)], 128 * B * 2 * 1.6)
    dma([(T.wI[:, 0:6], T.w[:]), (T.thI[0:1, 0:48], T.th[:])], [], [("wI", 0, 8), ("thI", 0, 48)], 4096)

    iota(col("pI", 0), [[0, 1]], 0, 1, False)
    iota(V("J"), [[1, 256]])
    iota(V("JB"), [[0, 16], [1, 16]])
    ts(col("pI", 1), col("pI", 0), 15, ALU.bitwise_and)
    ts(col("pI", 2), col("pI", 0), 4, ALU.arith_shift_right)
    cp(V("pF", 0, 3), V("pI", 0, 3))
    pr, pg = col("pF", 1), col("pF", 2)
    ts(col("pF", 3), col("pF", 0), 16.0, ALU.add)
    ts(V("IW"), V("J", 0, 176), col("pF", 3), ALU.is_equal)
    ts(V("RM"), V("J", 0, 16), pr, ALU.is_equal)
    IH = V("IW", 16, 144)
    ts(V("pF", 4, 8), V("J", 0, 16, 4), 1.0, ALU.add, pr, ALU.is_le)
    tt(V("pF", 8, 11), V("pF", 4, 7), V("pF", 5, 8), ALU.subtract)
    for p, c in enumerate((10, 7, 8, 9)):
        ts(V("MP", 176 * p, 176 * p + 176), V("IW"), col("pF", c), ALU.mult)
    for r in range(16):
        ts(V("W16", 144 * r, 144 * r + 144), V("IW", r + 1, r + 145), col("RM", r), ALU.mult)
    w16 = lambda r, b: V("W16", 144 * r + 15 - b, 144 * r + 143 - b)
    iota(V("KB", 0, B), [[0, B // 8], [1, 8]])
    ops[-1]["rd"] = [("JB", 0, 256), ("J", 0, 256)]
    for q in range(4):
        cp(V("K0", qb * q, qb * q + qb), V("kint", qb * q, qb * q + qb))

    def kbcopy(src, o, c0, c1):
        dma([(T.KB[r:128:16, c0:c1], T[src][r:128:16, o + c0:o + c1]) for r in range(6)],
            [(src, o + c0, o + c1)], [("KB", c0, c1)], 48 * (c1 - c0) * 4)
    kbcopy("K0", 0, 0, B)
    dma([(T.K[:, PAD:PAD + B], T.K0[:]), (T.K[:, 0:PAD], T.K0[:, 0:PAD])], [("K0", 0, B), ("KB", 0, B)], [("K", 0, PAD + B)],
        128 * B * 4)
    ts(col("pF", 11), pr, 8.0, ALU.mult, pg, ALU.add)
    ts(V("SEL"), V("J", 0, 128), col("pF", 11), ALU.is_equal, 0.0625, ALU.mult)
    ts(V("Blk"), V("J", 0, 8), pg, ALU.is_equal)
    blk = V("Blk")
    act(V("Ib"), IH)
    scale(V("nIb"), IH, -1.0)
    scale(V("RR", 0, 16, 2), blk, 4096.0)
    scale(V("RR", 1, 16, 2), blk, 4096.0)
    scale(V("I16"), IH, 16.0)
    ts(col("pF", 12), pr, 6.0, ALU.is_le, BIG, ALU.mult)
    ts(V("RR", 16, 32), V("RR", 0, 16), 0.0, ALU.is_gt, col("pF", 12), ALU.mult)
    scale(V("RR", 32, 48), V("RR", 0, 16), -1.0)
    scale(V("RR", 48, 64), V("RR", 0, 16), 2.0)
    rs, rb, rn, r2 = (V("RR", 16 * j, 16 * j + 16) for j in range(4))
    ms(V("oneb", p=one), 1.0)
    ones = V("oneb", p=one)
    iota(V("kc", p=one), [[-2048, 2], [0, 32], [256, 8]], 2304)
    psel(V("kc", 0, 256, p=one), V("kc", 0, 256, p=one), [[0, 32], [-1, 8]], 6)
    iota(V("tmpc", 0, 128), [[1, 8], [0, 16]])
    ts(V("nBR"), V("tmpc", 0, 128), pg, ALU.is_equal, -1.0, ALU.mult)
    scale(V("RX"), V("nBR"), 4096.0)
    ms(V("rst"), -1e9)
    ms(V("rst", 0, 256, 8), 16777216.0)
    for d in (1, 2, 3):
        send(rank - d, V("XQ%d" % d, 0, B), V("X", 0, B), "xi%d" % d)
        ops[-2]["rd"] = ops[-2]["rd"] + [("KB", 0, B)] + ([("scn", 0, 256)] if d > 1 else [])
    iota(V("KB", B, W), [[0, (W - B) // 8], [1, 8]])

    def late_constants():
        scale(V("hIb"), IH, 0.5)
        act(V("I32"), IH)
        cp(V("Blk16"), blk)
        act(V("Blkb"), blk)
        scale(V("RR", 64, 72), blk, 16.0)
        cp(V("repl"), V("J", 0, 16))
        ts(V("rep4"), V("J", 0, 16), 4.0, ALU.mult, 3.0, ALU.add)
        ms(V("o4k"), 4096.0)
        ts(V("Dm"), V("JB"), pr, ALU.is_equal)
        ts(V("wt"), V("JB"), pr, ALU.is_gt)
        scale(V("pk"), V("Dm"), EW)
        tt(V("wt"), V("wt"), V("pk"), ALU.add)
        ts(V("Mm"), V("JB"), pr, ALU.is_le, 8192.0, ALU.mult)
        ms(V("rsa"), 0.0)
        ms(V("rsa", 0, 128, 16), 1e9)
        ms(V("sd"), -1.0)
        ms(V("sd", 0, 64, 4), 0.0)
        ms(V("sd", 2, 64, 4), -16.0)
        ts(col("pF", 13), pg, 8.0, ALU.add)
        for j, (cmp, c) in enumerate(((ALU.is_equal, pg), (ALU.is_equal, col("pF", 13)), (ALU.is_gt, pg), (ALU.is_gt, col("pF", 13)))):
            ts(V("RE", 48 * j, 48 * j + 16), V("JB", 0, 16), c, cmp, 1.0 / 4096, ALU.mult)
            ts(V("RE", 48 * j + 16, 48 * j + 48), V("JB", 0, 32), c, cmp, -1.0, ALU.mult)
        ts(V("CE", 48, 64), V("J", 0, 16), 16.0, ALU.mult, pr, ALU.add)
        act(V("CE", 0, 16), V("CE", 48, 64), AF.Copy, -(0.5 - 1.0 / 8192), 3.0)
        act(V("CE", 16, 48), V("J", 0, 32), AF.Copy, EW + 255.0, 0.0)
        act(V("MZ", 16, 32), V("CE", 48, 64), AF.Copy, 256.0)
        scale(V("CE", 48, 64), V("CE", 48, 64), 16.0)
        act(V("J16"), V("J"))
        act(V("kca", p=one), V("JB", 0, 128, p=one))
        ms(V("qc", p=one), -0.25)
        ms(V("qc", 256, 272, p=one), 1920.0 / 4096)
        cm = lambda j: V("CM", 128 * j, 128 * j + 128)
        r67, n67 = col("pF", 14), col("pF", 15)
        tt(r67, col("RM", 6), col("RM", 7), ALU.add)
        ts(n67, r67, -1.0, ALU.mult, 1.0, ALU.add)
        grp(V("pT2", 0, 128), [(IH, w16(0, 2)), (IH, w16(1, 3)), (IH, w16(7, 8))])
        act(cm(0), V("pT2", 0, 128))
        grp(V("pT2", 128, 256), [(IH, w16(0, 4)), (IH, w16(1, 5)), (IH, V("MP", 16, 144)), (IH, V("MP", 192, 320))])
        act(V("CM32"), V("pT2", 128, 256))
        ts(col("pF", 16), col("RM", 0), 8.0, ALU.mult, r67, ALU.add)
        ts(cm(1), IH, col("pF", 16), ALU.mult)
        ts(cm(2), IH, n67, ALU.mult)
        ts(col("pF", 17), col("RM", 6), 8.0, ALU.mult, col("RM", 7), ALU.add)
        scale(V("VN"), V("J"), col("pF", 17))
        ts(V("pF", 24, 30), V("RM", 9, 15), -1.0, ALU.mult, 1.0, ALU.add)
        for t in range(R):
            ts(V("CA", 128 * t, 128 * t + 128), IH, col("pF", 24 + t), ALU.mult)
        j6 = V("J", 0, 6)
        c18, c19, c20 = col("pF", 18), col("pF", 19), col("pF", 20)
        ts(c18, col("RM", 0), col("RM", 1), ALU.add)
        ts(c18, r67, 256.0, ALU.mult, c18, ALU.add)
        ts(c19, col("RM", 2), col("RM", 3), ALU.add, col("RM", 8), ALU.add)
        ts(c19, c19, 2048.0, ALU.mult)
        ts(c19, r67, float(B), ALU.mult, c19, ALU.add)
        ts(c19, col("RM", 1), float(MID), ALU.mult, c19, ALU.add)
        ts(V("BI", 0, 6), j6, c18, ALU.mult, c19, ALU.add)
        ts(c18, col("RM", 7), 256.0, ALU.mult, col("RM", 6), ALU.add)
        ts(c20, col("RM", 7), float(B), ALU.mult)
        ts(V("BI", 16, 22), j6, c18, ALU.mult, c20, ALU.add)
        ts(c19, col("RM", 6), float(MID), ALU.mult)
        ts(c19, n67, 2048.0, ALU.mult, c19, ALU.add)
        ts(V("BI", 8, 14), V("BI", 16, 22), c19, ALU.add)
        ts(V("BI", 24, 30), j6, 256.0, ALU.mult, 256.0, ALU.add)
        tt(V("BI", 24, 30), V("BI", 24, 30), V("RM", 9, 15), ALU.mult)
        ts(V("BI", 24, 30), V("BI", 24, 30), 2048.0, ALU.add)
        ms(V("E", 0, 512), 0.0)
        dma([(T.E[:, 512 * q:512 * q + 512], T.E[:, 0:512]) for q in range(1, 8)], [("E", 0, 512)], [("E", 512, 4096)], 128 * 7168)
        iota(V("pc"), [[0, 512]])
        ms(V("bJ"), 0)
        ts(V("thF", p=one), V("thI", p=one), 4081.0, ALU.min, 4096.0, ALU.mult)
        add("pool", lambda g: g.partition_broadcast(T.thB[:], T.thF[0:1, :], 128), [("thF", 0, 48)], [("thB", 0, 48)],
            (140, 192, 0, 0, 0, 0))
        for h in range(2):
            act(V("thz", 8 * h, 8 * h + 8), V("thB", 0, 48, 6), AF.Copy, -128.0)
        act(V("thB"), V("thB"), AF.Copy, 30720.0 - 128.0)
        cp(V("wF", 0, 6), V("wI", 0, 6))
        for t in range(R):
            scale(V("wS", 8 * t, 8 * t + 8), blk, col("wF", t))
        mm([(V("pT3", 16 * t + 8 * h, 16 * t + 8 * h + 8), xv(t, h), V("wS", 8 * t, 8 * t + 8), True, True)
            for t in range(R) for h in range(2)])
        cp(V("aI"), V("pT3", 0, 96))
        ts(V("aJ"), V("aI"), 2047, ALU.bitwise_and)
        asklists(1)

    def asklists(d):
        for j in range(2):
            t = d - 1 + 3 * j
            tt(V("aL"), IND(V("aJ", 16 * t, 16 * t + 16), V("repl")), V("Dm"), ALU.mult)
            mm([(V("pT3", 128 + 16 * j + 8 * h, 136 + 16 * j + 8 * h), V("aL", 128 * h, 128 * h + 128), V("Blk16"), True, True)
                for h in range(2)])
        cp(V("aU", 32 * d - 32, 32 * d), V("pT3", 128, 160))
        send(rank + d, V("aR", 32 * d - 32, 32 * d), V("aU", 32 * d - 32, 32 * d), "al%d" % d, 4)

    def lanes(name, t, h=None):
        o = PAD if name == "K" else 0
        if h is None:
            return V(name, o + t, o + 2048, 8)
        return V(name, o + t + 1024 * h, o + 1024 * h + 1024, 8)

    def xv(t, h=None):
        return lanes("X", t, h)

    def spreads(t):
        for j, (name, src) in enumerate((("xvb", "X"), ("kvb", "KB"))):
            for kk in range(4):
                q = CFG["SP0"][4 * j + kk] if t == 0 else "p"
                {"p": pcopy, "a": act, "v": cp}[q](V(name + str(t % 2), kk, 1024, 4), lanes(src, t))

    def first_list(t, p, src, out):
        k0 = (9 + 4 * p) % 16
        pairs = []
        for lg in range(4):
            o = 176 * p + 16 - (4 * lg - k0)
            pairs.append((V("MP", o, o + 128), V(src, lg, 256, 4)))
            if p == 1:
                pairs.append((w16(0, 4 * lg + 3), V(src, lg, 256, 4)))
        grp(out, pairs)

    def still_lists(t):
        shifted("a", V("ks16"), lanes("K0", t), -2048.0)
        for p in range(3):
            first_list(t, p, "ks16", V("bF", 64 * p, 64 + 64 * p))
        o = 256 * (t % 2)
        ts(V("l1", o, o + 192), V("bF", 0, 192), 2048.0, ALU.add)

    def relatives(t, p):
        cnt = B + L * t
        still = p < 2 or t == 0 or (p == 2 and t == 1)
        win = V("K0") if still else Kp(0, cnt)
        bank = "bF" if p < 2 else "bD"
        o = 256 * (t % 2) + 64 * p
        if p == 3:
            shifted("v", V("kv16"), lanes("K0" if t == 0 else "K", t), -2048.0)
            first_list(t, p, "kv16", V(bank, 320, 384))
            ts(V("l1", o, o + 64), V(bank, 320, 384), 2048.0, ALU.add)
        for h in range(2):
            shifted(CFG["KG"][t][2 * p + h], V("G16", 1024 * p + 512 * h, 1024 * p + 512 * h + 512),
                    IND(win, V("l1", o + 32 * h, o + 32 * h + 32)), -float(MID + t))
        row = [(9 + 4 * p + kk + t) % 16 for kk in range(4)]
        lp = V(bank, 256 + 64 * (p % 2), 320 + 64 * (p % 2))
        for b0 in (0, 8):
            grp(lp, [(w16(row[b % 4], b), V("G16", 1024 * p + b, 1024 * p + 1024, 16)) for b in range(b0, b0 + 8)],
                b0 == 0, b0 == 8)
        ts(V("l2", 64 * p, 64 * p + 64), lp, float(MID + t), ALU.add)
        mm([(V(bank, 384 + 64 * h + 4 * (p % 2) + kk, 448 + 64 * h, 8),
             V("G16", 1024 * p + 512 * h + kk, 1024 * p + 512 * h + 512, 4), V("SEL", 8 * row[kk], 8 * row[kk] + 8), True, True)
            for h in range(2) for kk in range(4)])

    def split(t, s):
        bank = ("bF", "bD")[s]
        o = 256 if s else 128 * (t % 2)
        ts(V("hi", o, o + 128), V(bank, 384, 512), MAG0, ALU.add, MAG0, ALU.subtract)
        tt(V("lo", o, o + 128), V(bank, 384, 512), V("hi", o, o + 128), ALU.subtract)
        mm([(V(("bS", "bD")[s], 0, 256), ones, V("kc", 256 * s, 256 * s + 256, p=one), True, False)])

    def payload(t, s, last):
        bank = ("bS", "bD")[s]
        o = 256 if s else 128 * (t % 2)
        for wi in range(2):
            mm([(V(bank, 8 * wi + j, 256, 16), V(("Ib", "I16")[wi]), V(("hi", "lo")[wi], o + j, o + 128, 8), False,
                 last and wi == 1 and j == 7) for j in range(8)])

    def room(t, p):
        return 1024 * (p + 2 * (t % 2) if p < 2 else p + 2)

    def keyed(p, h, name, o, rhs, last=False):
        bank = "bS" if p < 2 else "bD"
        mm([(V(bank, 128 * h + 4 * (p % 2) + kk, 128 * h + 128, 8), V(name, o + 512 * h + kk, o + 512 * h + 512, 4), rhs,
             False, last and kk == 3) for kk in range(4)])

    def blood(t, p):
        wn = B if p < 2 or t == 0 or (p == 2 and t == 1) else B + L * t
        for h in range(2):
            c = room(t, p) + 512 * h
            tt(V("eq", c, c + 512), IND(V("KB", 0, wn), V("l2", 64 * p + 32 * h, 64 * p + 32 * h + 32)),
               V("kvb%d" % (t % 2), 512 * h, 512 * h + 512), ALU.is_equal)

    def feats(t, p):
        wn = B if p < 2 or t == 0 or (p == 2 and t == 1) else B + L * t
        xvb = "xvb%d" % (t % 2)
        for h in range(2):
            c = room(t, p) + 512 * h
            dab = V("Dab", 1024 * p + 512 * h, 1024 * p + 512 * h + 512)
            src = IND(V("X", 0, wn), V("l2", 64 * p + 32 * h, 64 * p + 32 * h + 32))
            rt = CFG["XR"][t][2 * p + h]
            if rt == "d":
                tt(V("Xc", c, c + 512), src, V(xvb, 512 * h, 512 * h + 512), ALU.subtract)
                ts(dab, V("Xc", c, c + 512), 0.0, ALU.max, 2.0, ALU.mult)
                continue
            bank = ("pX1", "pX2")[h]
            if rt in "av":
                mm([(V(bank), V("nIb"), V(xvb, 512 * h, 512 * h + 512), True, False)])
            (act if rt in "af" else cp)(V("Xc", c, c + 512), src)
            if rt in "av":
                mm([(V(bank), V("Ib"), V("Xc", c, c + 512), False, True)])
                act(dab, V(bank), AF.Abs)
        if CFG["XR"][t][2 * p] in "fg":
            o = 2048 * t + 1024 * p
            fold(V("Mx", o, o + 1024), V("Xc", room(t, p), room(t, p) + 1024), V(xvb), "%d_%d" % (t, p))

    def sums(t, p, last=False):
        for h in range(2):
            keyed(p, h, "eq", room(t, p), rb)
        for h in range(2):
            rt = CFG["XR"][t][2 * p + h]
            if rt in "dfg":
                keyed(p, h, "Xc", room(t, p), rn)
            if rt in "fg":
                keyed(p, h, "Mx", 2048 * t + 1024 * p, r2, last and h == 1)
            else:
                keyed(p, h, "Dab", 1024 * p, rs, last and h == 1)

    def still(t):
        still_lists(t)
        for p in range(2):
            relatives(t, p)
            feats(t, p)
            blood(t, p)
        split(t, 0)
        folded = [p for p in range(2) if CFG["XR"][t][2 * p] in "fg"]
        if len(folded) == 2:
            mm([(V("bS", 128 * h, 128 * h + 128), xv(t, h), V("RX"), False, False) for h in range(2)])
        elif folded:
            mm([(V("bS", 128 * h + 4 * folded[0] + kk, 128 * h + 128, 8), xv(t, h), rn, False, False)
                for h in range(2) for kk in range(4)])
        for p in sorted(range(2), key=lambda p: p in folded):
            sums(t, p)
        payload(t, 0, True)
        scan(V("scn", 256 * (t % 2), 256 * (t % 2) + 256), V("rst"), V("bS", 0, 256), ALU.max, ALU.min)

    def moving_a(t):
        relatives(t, 2)
        feats(t, 2)
        blood(t, 2)

    def moving_b(t):
        relatives(t, 3)
        blood(t, 3)
        split(t, 1)
        payload(t, 1, False)
        sums(t, 2)

    def moving_c(t):
        feats(t, 3)
        sums(t, 3, True)

    def wed(t):
        cnt = B + L * t
        off = float(MID + t)
        kt = "K0" if t == 0 else "K"
        kwin = lambda n: V("K0", 0, n) if t == 0 else Kp(0, n)
        d = t % 3 + 1
        cm = lambda j: V("CM", 128 * j, 128 * j + 128)
        ul = lambda j: V("uL", 16 * j, 16 * j + 16)
        ac = 32 * d - 32 + 16 * (t // 3)
        scale(V("dS", L * t, L * t + L), IND(kwin(2048), V("aR", ac, ac + 16)), 512.0)
        send(rank - d, V("dR", L * t, L * t + L), V("dS", L * t, L * t + L), "dq%d" % t, 8)
        if t < 2:
            asklists(t + 2)
        kv = lanes(kt, t)
        pcopy(V("pk"), xv(t))
        for nm, j in (("KW", 1), ("KW", 2), ("SW", 2)):
            pcopy(V(nm, j, 768, 3), kv)
        grp(V("pT3", 0, 256), [(V("CA", 128 * t, 128 * t + 128), V("kv16")), (w16(9 + t, 9 + t), V("J16"))])
        act(V("SW", 1, 768, 3), V("pT3", 0, 256), AF.Identity, col("BI", 24 + t))
        scan(V("scn", 512, 768), V("rst"), V("bD", 0, 256), ALU.max, ALU.min)
        tt(V("F", 1, 64, 2), V("scn", 256 * (t % 2) + 7, 256 * (t % 2) + 256, 8), V("scn", 519, 768, 8), ALU.min)
        ts(V("F", 0, 64, 2), V("F", 1, 64, 2), 256 * MAG0, ALU.add, 256 * MAG0, ALU.subtract)
        scan(V("mT"), V("sd"), V("F"), ALU.mult, ALU.add)
        act(V("LR"), IND(V("mT"), V("rep4")))
        tt(V("LM"), IND(V("mT"), V("rep4")), V("Dm"), ALU.mult)
        tt(V("nk"), V("F", 1, 64, 4), V("thz"), ALU.is_lt)
        mm([(V("pT1", 128 * h, 128 * h + 128), V("LR", 128 * h, 128 * h + 128), IH, True, True) for h in range(2)])
        mm([(V("pT3", 256 + 8 * h, 264 + 8 * h), V("LM", 128 * h, 128 * h + 128), V("Blk16"), True, True) for h in range(2)])
        mW = V("mW")
        act(V("mR"), V("pT1", 0, 256))
        ts(ul(0), V("pT3", 256, 272), off, ALU.add)
        cp(mW, V("pT3", 256, 272))
        mm([(V("pX1", 0, 256), V("Ib"), V("Mm"), True, False)]
           + [(V("pX1", 128 * h, 128 * h + 128), V(nm, 128 * h, 128 * h + 128), rh, False, nm == "LM" and h == 1)
              for nm, rh in (("LR", IH), ("LM", V("nBR"))) for h in range(2)])
        act(V("km"), IND(kwin(cnt), ul(0)), AF.Identity, col("BI", 16 + t), col("pF", 15))
        act(V("xm"), IND(V("X", 0, cnt), ul(0)))
        cP = lambda h: V("pT2", 8 * h, 8 * h + 8)
        Eh = lambda s, h: V("E", 256 * s + 128 * h, 256 * s + 128 * h + 128)
        b1 = V("Blkb")
        mm([(V("pT2", 0, 16), V("nIb"), V("nk"), True, False)])
        ts(V("E", 256 * 15, 256 * 16), V("pX1", 0, 256), 0.0, ALU.is_equal)
        mm([(cP(h), Eh(15, h), b1, False, False) for h in range(2)])
        for s in range(15):
            ts(V("E", 256 * s + 16 * s + 16, 256 * s + 256), V("mR", 16 * s + 16, 256), col("mW", s), ALU.is_equal)
            if s % 3 == 2:
                mm([(cP(h), Eh(u, h), b1, False, u == 14) for u in range(s - 2, s + 1) for h in range(2) if h == 1 or u < 7])
        act(V("MZ", 0, 16), mW, AF.Copy, off + PAD)
        eP = V("pT1", 256, 304)
        mm([(eP, V("I32"), V("CE", 0, 48), True, False)])
        ts(V("lost"), V("pT2", 0, 16), 0.0, ALU.is_ge)
        tt(V("Lw"), IND(V("lost"), V("repl")), V("wt"), ALU.mult)
        act(V("Lr"), IND(V("lost"), V("repl")))
        grp(eP, [(V(nm, 128 * h, 128 * h + 128), V("RE", o + 48 * h, o + 48 * h + 48))
                 for nm, o in (("Lw", 0), ("Lr", 96)) for h in range(2)], False, True)
        grp(V("pX2", 0, 256), [(cm(2), V("kv16")), (w16(7, 7), V("J16")), (w16(6, 6), V("mR"))])
        act(V("SW", 0, 768, 3), V("pX2", 0, 256), AF.Identity, col("BI", 8 + t))
        grp(V("pX2", 256, 512), [(cm(0), V("kv16")), (cm(1), V("J16")), (w16(1, 1), V("mR")), (V("CM32"), V("km"))])
        act(V("KW", 0, 768, 3), V("pX2", 256, 512), AF.Identity, col("BI", t))
        grp(V("pT3", 0, 256), [(ones, V("qc", 0, 256, p=one)), (V("hIb"), xv(t)), (V("hIb"), V("xm"))])
        if t < R - 1:
            ts(V("X", cnt, cnt + L), V("pT3", 0, 256), MAG0, ALU.add, MAG0, ALU.subtract)
            dma([(T.XW[:, 256:512], T.X[:, cnt:cnt + L])], [("X", cnt, cnt + L)], [("XW", 256, 512)], 65536)
        else:
            ts(V("XW", 256, 512), V("pT3", 0, 256), MAG0, ALU.add, MAG0, ALU.subtract)
        tt(V("zz"), V("pT1", 272, 304), V("MZ"), ALU.min)
        cp(V("uL", 32, 64), V("zz"))
        ts(ul(1), V("pT1", 256, 272), MAG0, ALU.add, MAG0, ALU.subtract)
        tt(IND(V("pc"), ul(3)), V("dR", L * t, L * t + L), V("pk"), ALU.add)
        act(lanes("K", t), IND(V("SW"), ul(1)))
        act(Kp(cnt, cnt + L), IND(V("KW"), ul(1)))
        tt(IND(V("K", 0, PAD + cnt), ul(2)), V("km"), V("VN"), ALU.add)
        if t < R - 1:
            kbcopy("K", PAD, cnt, cnt + L)
        pairs = [(yk[:, cnt:cnt + L], T.K[:, PAD + cnt:PAD + cnt + L]),
                 (yk[9 + t:128:16, 0:2048], T.K[9 + t:128:16, PAD:PAD + 2048])]
        nb = 128 * 1024 + 65536
        if t == R - 1:
            pairs += [(yk[r:128:16, 0:cnt], T.K[r:128:16, PAD:PAD + cnt]) for r in (6, 7)]
            nb += 16 * cnt * 4
        dma(pairs, [("K", 0, PAD + cnt + L)], [("yk", 0, W)], nb)

    def ask(t):
        cnt = B + L * t
        d = t % 3 + 1
        ts(V("dU"), V("pc", 192, 256), 1.0 / 512, ALU.mult)
        ts(V("pr"), V("pc", 192, 256), 512 * MAG0, ALU.add, 512 * MAG0, ALU.subtract)
        tt(V("xc"), V("pc", 192, 256), V("pr"), ALU.subtract)
        for c in range(2):
            (act if CFG["XA"][t][c] == "a" else cp)(V("Xa", 512 * c, 512 * c + 512),
                                                    IND(V("XQ%d" % d, 0, cnt), V("dU", 32 * c, 32 * c + 32)))
        lo = (0, 64)
        mm([(V("pT2", 0, 128, p=lo), V("oneb", 0, 64, p=one), V("kca", p=one), True, False)])
        for c in range(2):
            bank = ("pT3", "pT1")[c]
            mm([x for k in range(8 * c, 8 * c + 8) for x in
                ((V(bank, 64 * (k % 8), 64 * (k % 8) + 64), V("Ib"), V("Xa", k, 1024, 16), True, False),
                 (V(bank, 64 * (k % 8), 64 * (k % 8) + 64), V("nIb"), V("xc"), False, True))])
            act(V("Da", 512 * c, 512 * c + 512), V(bank), AF.Abs)
            mm([(V("pT2", k, 128, 16, p=lo), V("Da", 64 * k, 64 * k + 64), V("RR", 64, 72), False, k == 15)
                for k in range(8 * c, 8 * c + 8)])
        ts(V("pT3", 0, 192), V("pc", 0, 192), 512 * MAG0, ALU.add, 512 * MAG0, ALU.subtract)
        tt(V("XW", 0, 192), V("pc", 0, 192), V("pT3", 0, 192), ALU.subtract)
        if t < R - 1:
            grp(V("pT1", 0, 16), [(V("o4k", p=one), V("qc", 256, 272, p=one)), (V("o4k"), V("lost"))])
            add("dve", lambda g: g.vector.tensor_reduce(T.zF[:, 0:1], T.pT1[:, 0:16], AX.X, ALU.add),
                [("pT1", 0, 16)], [("zF", 0, 1)], (16, 64, 0, 0, 0, 0))
            ts(col("zF", 1), col("zF", 0), 65536 * MAG0, ALU.add, 65536 * MAG0, ALU.subtract)
            for h in range(2):
                ts(V("thz", 8 * h, 8 * h + 8), V("thB", t + 1, 48, 6), col("zF", 1), ALU.add, col("zF", 0), ALU.subtract)
        scan(V("asn", p=lo), V("rsa", p=lo), V("pT2", 0, 128, p=lo), ALU.add, ALU.min)
        cp(V("bI", p=lo), V("asn", 15, 128, 16, p=lo))
        ts(V("bJ", p=lo), V("bI", p=lo), 15, ALU.bitwise_and)
        tt(V("bL"), IND(V("bJ"), V("repl", 0, 8)), V("Dm", 0, 128), ALU.mult)
        grp(V("pT2", 256, 260), [(V("I32"), V("CE", 48, 52)), (V("bL", p=lo), V("Blk16", 0, 4, p=lo))])
        cp(V("uL", 64, 68), V("pT2", 256, 260))
        act(V("XW", 192, 256), IND(V("Xa"), V("uL", 64, 68)))
        act(V("X", cnt, cnt + L), IND(V("XW"), V("uL", 48, 64)))
        for u, dd in sorted(XSEND, key=lambda x: (x[1] - (t + 1) % 3 - 1) % 3):
            if u == t:
                send(rank - dd, V("XQ%d" % dd, cnt, cnt + L), V("X", cnt, cnt + L), "xn%d_%d" % (u, dd), 8)
        dma([(yx[:, L * t:L * t + L], T.X[:, cnt:cnt + L])], [("X", cnt, cnt + L)], [("yx", L * t, L * t + L)], 65536)

    spreads(0)
    still(0)
    late_constants()
    moving_a(0)
    moving_b(0)
    dma([(yk[:, 0:B], T.K0[:])], [("K0", 0, B), ("eq", 5120, 5632)], [("yk", 0, W)], 128 * B * 4)
    for t in range(R):
        moving_c(t)
        if t + 1 < R:
            spreads(t + 1)
            still(t + 1)
        wed(t)
        if t + 1 < R:
            moving_a(t + 1)
            moving_b(t + 1)
        ask(t)
    return ops


def depend(ops):
    hist = {}
    for o in ops:
        dep = {}
        if "after" in o:
            dep[o["after"]] = True
        acc = [(r, False) for r in o["rd"]] + [(r, True) for r in o["wr"]]
        acc = [(r[0], r[1], r[2], r[3] if len(r) > 3 else 1, w) for r, w in acc]
        for name, a, b, st, w in acc:
            for (a2, b2, w2, j, st2) in hist.get(name, []):
                if j == o["id"]:
                    continue
                if name in PS:
                    dep[j] = dep.get(j, False) or ops[j]["eng"] != o["eng"] or (o["eng"] != "pe" and (w or w2))
                elif (w or w2) and a < b2 and a2 < b and (st != st2 or (a - a2) % st == 0):
                    dep[j] = True
        for name, a, b, st, w in acc:
            hs = hist.setdefault(name, [])
            if name in PS:
                if any(ops[x[3]]["eng"] != o["eng"] for x in hs):
                    hs[:] = [x for x in hs if x[3] == o["id"]]
            elif w and st == 1:
                hs[:] = [x for x in hs if not (a <= x[0] and x[1] <= b) or x[3] == o["id"]]
            hs.append((a, b, w, o["id"], st))
        o["dep"] = dep


def place(ops, cost, hop, seq, pred, back):
    t0 = [0.0] * len(ops)
    gaps = {e: [[0.0, 1e12]] for e in ENG}
    end = 0.0
    for i in seq:
        o = ops[i]
        c, lat = cost[i], o.get("lat", 0.0)
        r = lat if back else 0.0
        for j, hard in pred[i]:
            x = t0[j] + cost[j]
            if hard:
                x += hop + (lat if back else ops[j].get("lat", 0.0))
            r = max(r, x)
        if o["eng"] != "recv":
            gl = gaps[o["eng"]]
            k = len(gl) - 1
            while k > 0 and gl[k - 1][1] >= r + c:
                k -= 1
            while max(gl[k][0], r) + c > gl[k][1]:
                k += 1
            a, b = gl[k]
            r = max(a, r)
            gl[k:k + 1] = [x for x in ([a, r], [r + c, b]) if x[1] - x[0] > 40.0 or x[1] > 1e11]
        t0[i] = r
        end = max(end, r + c + (0.0 if back else lat))
    return t0, end


def replay(ops, cost, hop, order, pred):
    free = {}
    t1 = [0.0] * len(ops)
    for i in order:
        e = ops[i]["eng"]
        r = free.get(e, 0.0)
        for j, hard in pred[i]:
            if hard and t1[j] + hop > r:
                r = t1[j] + hop
        if e != "recv":
            free[e] = r + cost[i]
        t1[i] = r + cost[i] + ops[i].get("lat", 0.0)
    return max(t1)


def improve(ops, rounds=300):
    n = len(ops)
    pred = [list(o["dep"].items()) for o in ops]
    succ = [[] for _ in range(n)]
    for o in ops:
        for j, hard in o["dep"].items():
            succ[j].append((o["id"], hard))
    cost = [price(o, NOMINAL) for o in ops]
    hop = NOMINAL[4]
    more = [([price(o, m) for o in ops], m[4], m[0]) for m in OTHERS]
    prio = [0.0] * n
    for i in range(n - 1, -1, -1):
        prio[i] = cost[i] + ops[i].get("lat", 0.0) + max([prio[k] + (hop if h else 0.0) for k, h in succ[i]] + [1e-3])
    seq = sorted(range(n), key=lambda i: (-prio[i], i))
    best = None
    x = [12345]

    def rnd():
        x[0] = (x[0] * 1103515245 + 12345) % 2147483648
        return x[0] / 2147483648.0
    for it in range(rounds):
        t0, end = place(ops, cost, hop, seq, pred, False)
        if best is None or end < best[2] * 1.02:
            order = sorted(range(n), key=lambda i: (t0[i], i))
            val = end / NOMINAL[0] + sum(replay(ops, c, h, order, pred) / f for c, h, f in more)
            if best is None or val < best[0]:
                best = (val, t0, end, order)
        if it % 4 == 3:
            lo = rnd() * best[2]
            key = [0.0] * n
            for i in range(n):
                k = best[1][i]
                if lo <= k < lo + 30000.0:
                    k += (rnd() - 0.5) * 3000.0
                key[i] = max([k] + [key[j] + 1e-3 for j, _h in pred[i]])
            seq = sorted(range(n), key=lambda i: (key[i], i))
            continue
        seq = sorted(range(n), key=lambda i: (-(t0[i] + cost[i] + ops[i].get("lat", 0.0)), -i))
        tb, _e = place(ops, cost, hop, seq, succ, True)
        seq = sorted(range(n), key=lambda i: (-(tb[i] + cost[i]), i))
    for o in ops:
        o["t0"] = best[1][o["id"]]
        o["t1"] = o["t0"] + cost[o["id"]] + o.get("lat", 0.0)
    return best[3]


ORDER = {}


def ordered(T, topo, core, rank):
    ops = build(T, topo, core, rank)
    depend(ops)
    if "all" not in ORDER:
        ORDER["all"] = improve(ops)
    return ops, ORDER["all"]


def hand_back(g, core, T, topo, rank):
    dst = T.cores[rank]
    rid, pid = topo.addr(dst)[:2]
    sent = 0
    for t in range(R):
        for p in range(2):
            if CFG["XR"][t][2 * p] in "fg":
                tag = "%d_%d" % (t, p)
                blk = T.Mx[:, 2048 * t + 1024 * p:2048 * t + 1024 * p + 1024]
                g.wait_ge(T.sem["fo" + tag], 16)
                g.remote_dma(blk, blk, T.sem["fb" + tag], T.sem.sent, pid, rid, mask_of(topo, core, dst, 16))
                sent += 16
    if sent:
        g.wait_ge(T.sem.sent, sent)


def rank_program(g, core, T, topo):
    rank = T.rank_of(core)
    if rank is None:
        for r, c in enumerate(T.cores):
            if core in topo.cores_of(c) and helper_of(T, topo, c) == core:
                hand_back(g, core, T, topo, r)
        return
    ops, order = ordered(T, topo, core, rank)
    queue = {"pe": g.tensor, "dve": g.vector, "act": g.scalar, "pool": g, "sp": g.sync}
    needed = set(j for o in ops for j, hard in o["dep"].items() if hard)
    count = {e: 0 for e in ENG}
    mark = {}
    seen = {e: {} for e in ENG}
    sent = 0
    for i in order:
        o = ops[i]
        e = o["eng"]
        if e == "recv":
            mark[i] = (o["sem"], o["cnt"])
            continue
        want = {}
        for j, hard in o["dep"].items():
            if hard and j in mark:
                s, v = mark[j]
                want[s] = max(want.get(s, 0), v)
        for s, v in want.items():
            if seen[e].get(s, 0) < v:
                queue[e].wait_ge(T.sem[s], v)
                seen[e][s] = v
        ins = o["fn"](g)
        if "sem" in o:
            mark[i] = (o["sem"], o["cnt"])
        elif "rem" in o:
            sent += o["rem"]
        elif i in needed:
            count[e] += 1
            ins.then_inc(T.sem["c_" + e], 1)
            mark[i] = ("c_" + e, count[e])
    final = {}
    for s, v in mark.values():
        final[s] = max(final.get(s, 0), v)
    final["sent"] = sent
    for s, v in final.items():
        if max(seen[e].get(s, 0) for e in ENG) < v:
            g.sync.wait_ge(T.sem[s], v)
